import numpy as np, ml_dtypes
CORES = [9,25,41,57]
N = 4
BF = ml_dtypes.bfloat16
W, RO, F, INV = 4032, 4, 1, 0
def rises(g):
    return np.sum(g > np.arange(W), axis=-1)
def perms(rng, *shape):
    return np.argsort(rng.random(shape + (W,)), axis=-1)
def some(rng, m):
    a = np.arange(W); s = rng.permutation(W)[:m]; a[s] = rng.permutation(s)
    return a
def turned(p):
    return W - 1 - np.argsort(p)[::-1]
def lower(rng, p):
    a = np.arange(W); b = np.argsort(p); v = int(rng.choice(np.flatnonzero((p > a) & (b < a))))
    q = p.copy(); q[b[v]] = p[v]; q[v] = v
    return q
def pack(g):
    return {"g0": np.ascontiguousarray(g.reshape(N, 128, W)).astype(np.int32)}
def setup_inputs(rng):
    g = perms(rng, N, 8, 16); part = rng.random((N, 8, 16)) < 0.4
    for q, k, i in np.argwhere(part):
        g[q, k, i] = some(rng, int(W * (0.3 + 0.7 * rng.random())))
    return pack(g)
def setup_inputs_ties(rng):
    g = perms(rng, N, 8, 16)
    for k in range(4):
        b = int(rng.integers(1, 9)); o = rng.permutation(W); pr = o[:2 * b].reshape(b, 2); rings = [np.sort(x) for x in np.array_split(o[2 * b:], b)]
        for q in range(N):
            top = int(rng.integers(0, 16))
            for i in range(16):
                if i != top and rng.random() < 0.2: continue
                a = np.arange(W); swap = i == top or rng.random() < 0.5
                for s in rings: a[s] = np.roll(s, -1 if i == top else -int(rng.integers(2, 61)))
                if swap: a[pr[:, 0]] = pr[:, 1]; a[pr[:, 1]] = pr[:, 0]
                g[q, k, i] = a
    for k in range(4, 8):
        for q in range(N):
            j = int(np.argmax(rises(g[q, k]))); i = (j + int(rng.integers(1, 16))) % 16
            g[q, k, i] = turned(g[q, k, j])
    return pack(g)
def setup_inputs_ends(rng):
    a = np.arange(W); x = a.copy(); x[0] = W - 1; x[W - 1] = 0
    kinds = np.stack([a, a[::-1], np.roll(a, -1), np.roll(a, 1), x]); p = perms(rng, N, 8, 16)
    g = np.where((rng.random((N, 8, 16)) < 0.4)[..., None], p, kinds[rng.integers(0, 5, (N, 8, 16))])
    o = rng.permutation(8)
    g[:, o[0]] = a
    g[:, o[1]] = p[:, o[1]]; g[rng.integers(0, N), o[1]] = a
    g[:, o[2]] = p[:, o[2]]; g[::2, o[2], 15] = kinds[2]; g[1::2, o[2], 0] = kinds[2]
    g[:, o[3]] = p[:, o[3]]
    for q in range(N):
        m = g[q, o[3]].copy(); j = int(np.argmax(rises(m)))
        if q % 2 == 0:
            m[[j, 15]] = m[[15, j]]; c = int(rises(m[15])); m[0] = lower(rng, turned(m[15]))
            for i in range(1, 15):
                if int(rises(m[i])) == c: m[i] = lower(rng, m[i])
        else:
            m[[0, j]] = m[[j, 0]]; u = int(np.argmax(m[0])); w = int(m[0, W - 2]); m[0, u] = w; m[0, W - 2] = W - 1
            m[1] = turned(m[0]); y = m[1].copy()
            s = np.flatnonzero((a < W // 2) & (y >= W // 2)); y[s] = y[rng.permutation(s)]
            m[int(rng.integers(2, 16))] = y
        g[q, o[3]] = m
    return pack(g)
def setup_inputs_grow(rng):
    g = np.zeros((N, 8, 16, W), np.int64); m = np.exp2(1 + (np.log2(W) - 3) * rng.random((N, 8, 16))).astype(np.int64)
    for q, k, i in np.ndindex(N, 8, 16): g[q, k, i] = some(rng, int(m[q, k, i]))
    return pack(g)
def setup_inputs_alike(rng):
    p = perms(rng, N, 8, 3); p[:, :3] = p[0, :3].copy(); p[:, :, 2] = np.argsort(p[:, :, 1], axis=-1)
    g = np.take_along_axis(p, rng.integers(0, 3, (N, 8, 16))[..., None], 2)
    g[:, 7] = g[:, 7, :1].copy()
    h = W // 2 - 1
    for q in range(N):
        o = rng.permutation(W); s = np.sort(o[:h]); z = np.sort(o[h:2 * h])
        a = np.arange(W); a[s] = np.roll(s, -1); a[z] = np.roll(z, 1); b = some(rng, W // 8)
        k = rng.integers(0, 3, 16); k[rng.integers(0, 16)] = 0
        g[q, 5] = np.stack([a, b, np.argsort(b)])[k]
    o = 1 + rng.permutation(W - 3); m = W // 2
    up = np.sort(np.append(o[:m - 2], [0, W - 2])); down = np.sort(np.append(o[m - 2:], [W - 1]))[::-1]; nxt = np.roll(down, -1)
    one = np.zeros(W, np.int64); one[up] = down; one[down] = up
    two = np.zeros(W, np.int64); two[up] = nxt; two[nxt] = up
    r = int(rng.integers(0, N)); g[:, 6] = np.roll(np.arange(W), -1); g[r, 6] = one; g[(r + 1 + F) % N, 6] = two
    return pack(g)
def setup_inputs_spread(rng):
    g = np.zeros((N, 8, 16, W), np.int64)
    for q, k, i in np.ndindex(N, 8, 16):
        m = max(2, min(W, int(np.exp2(1 + (np.log2(W) - 1) * rng.random()) + 0.5)))
        if rng.random() < 0.5:
            s = np.sort(rng.permutation(W)[:m]); u = rng.random(); a = np.arange(W); a[s] = np.roll(s, -min(m - 1, 1 + int((m - 1) * u * u * u))); g[q, k, i] = a
        else: g[q, k, i] = some(rng, m)
    return pack(g)
def check_inputs(d):
    a = np.asarray(d["g0"])
    if a.shape != (N, 128, W) or np.any(np.sort(a, axis=-1) != np.arange(W)): return ["rows of g0 are permutations"]
    return []
def reference(g0):
    g = g0.astype(np.int64).reshape(N, 8, 16, W); e = rises(g)
    for t in range(RO):
        J = np.argmax(e, axis=2)
        L = np.take_along_axis(g, J[:, :, None, None], 2)
        for s in range(F + 1):
            if s == 0: M = L
            else: M = L[np.array([(r + 1 + (t * F + s - 1) % (N - 1)) % N for r in range(N)])]
            ix = np.broadcast_to(M, g.shape)
            if s > 0 and INV:
                h = np.zeros_like(g); np.put_along_axis(h, ix, g, 3)
            else: h = np.take_along_axis(g, ix, 3)
            eh = rises(h); up = eh > e
            g = np.where(up[..., None], h, g); e = np.where(up, eh, e)
    return {"yg": g.reshape(N, 128, W).astype(np.float32), "ye": e.reshape(N, 128, 1).astype(np.float32)}

@@ -1,0 +1,388 @@
+from concourse.mybir import AluOpType, AxisListType, ActivationFunctionType
+
+W = 4032
+RO = 4
+KB = W // 16
+C = 0.021
+MID = 2016.0
+MAGIC = 12582912.0
+NR = 96
+
+PAR = {
+    "load": [0, 1888, 3040, 3744, 4032],
+    "sub": [0, 608, 1248, 1888, 2464, 3040, 3392, 3744, 4032],
+    "eb": [0, 1184, 2464, 4032],
+    "e0": [("em", 0, 3), ("tv", 0, 640), ("tv", 3168, 4032), ("el", 0, 3), ("er", 0)],
+    "g0": [("em", 1, 0), ("em", 2, 1), ("tg", 0, 640), ("gs", 640, 1184), ("el", 1, 0), ("er", 1), ("gs", 1728, 2464),
+           ("c", 640, 1184), ("gv", 1184, 1728), ("el", 2, 1), ("er", 2), ("c", 1184, 2464), ("gs", 2464, 3200),
+           ("c", 2464, 3200), ("gs", 3200, 3680), ("c", 3200, 3680), ("gs", 3680, 3936), ("c", 3680, 3936),
+           ("gs", 3936, 4032), ("c", 3936, 4032), ("gs", 0, 640)],
+    "g1": [("tg", 3168, 4032), ("gv", 0, 224), ("c", 0, 224), ("gs", 224, 1472), ("c", 224, 1472), ("gs", 1472, 2272),
+           ("c", 1472, 2272), ("gs", 2272, 2784), ("c", 2272, 2784), ("gs", 2784, 3072), ("c", 2784, 3072),
+           ("gs", 3072, 3168), ("c", 3072, 3168), ("gs", 3168, 4032)],
+    "s0": [("pe", 1568, 1888, 0, "s"), ("vb", 0, 1568), ("va", 0, 1568), ("vc", 0, 1568), ("pe", 1888, 2336, 1, "s"),
+           ("pe", 2336, 2816, 2, "s"), ("pe", 2816, 3264, 3, "s"), ("pe", 3264, 3744, 0, "s"), ("pe", 3744, 4032, 1, "v")],
+    "s1": [("k0",), ("pe", 0, 416, 0, "s"), ("pe", 416, 800, 1, "s"), ("k1",), ("vb", 2176, 4032), ("k2",),
+           ("va", 2176, 4032), ("vc", 2176, 4032), ("pe", 800, 1216, 2, "s"), ("pe", 1216, 1632, 0, "s"),
+           ("pe", 1632, 2048, 1, "s"), ("em", 0, 3), ("el", 0, 3), ("pe", 2048, 2176, 2, "s"), ("er", 0)],
+    "fin": [(0, 256, "v"), (256, 704, "v"), (704, 1184, "v"), (1184, 1664, "s"), (1664, 2112, "v"), (2112, 2592, "s"),
+            (2592, 3072, "s"), (3072, 3552, "s"), (3552, 4032, "s")],
+    "store": [256, 704, 1184, 2112, 3072, 4032],
+    "yek": 7,
+}
+
+SCRATCH = {
+    "raw": ("sbuf", [128, W], "int32"),
+    "lin": ("sbuf", [128, W], "float32"),
+    "p": ("sbuf", [128, W], "bfloat16"),
+    "h": ("sbuf", [128, W], "bfloat16"),
+    "cmp": ("sbuf", [128, W], "bfloat16"),
+    "ths": ("sbuf", [128, W], "bfloat16"),
+    "seed": ("sbuf", [128, 32, 8], "float32"),
+    "wide": ("sbuf", [128, 32, 128], "bfloat16"),
+    "dif": ("sbuf", [128, 128], "float32"),
+    "ci": ("sbuf", [128, 288], "int32"),
+    "cj": ("sbuf", [128, 288], "int32"),
+    "X": ("sbuf", [128, 256], "bfloat16"),
+    "DX": ("sbuf", [128, 256], "bfloat16"),
+    "I128": ("sbuf", [128, 128], "bfloat16"),
+    "negI": ("sbuf", [128, 128], "float32"),
+    "G": ("sbuf", [128, 128], "float32"),
+    "M16": ("sbuf", [128, 16], "float32"),
+    "rk": ("sbuf", [128, 16], "float32"),
+    "Zoff": ("sbuf", [128, 144], "bfloat16"),
+    "Z": ("sbuf", [128, 144], "bfloat16"),
+    "Kb": ("sbuf", [128, 24], "float32"),
+    "sm": ("sbuf", [128, 16], "float32"),
+    "nb": ("sbuf", [128, 16], "bfloat16"),
+    "ec": ("sbuf", [128, 4], "float32"),
+    "lnx": ("sbuf", [128, 256], "float32"),
+    "thr": ("psum", [128, 4096], "bfloat16"),
+    "b0": ("psum", [128, 512], "float32"),
+    "b1": ("psum", [128, 512], "float32"),
+    "b2": ("psum", [128, 512], "float32"),
+    "b3": ("psum", [128, 512], "float32"),
+}
+for _t in range(RO):
+    SCRATCH["off%d" % _t] = ("sbuf", [128, 256], "uint16")
+    SCRATCH["land%d" % _t] = ("sbuf", [128, 256], "uint16")
+
+SEMAPHORES = (["cv", "cs", "cp", "cg", "sent", "stored"] + ["arr%d" % t for t in range(RO)]
+              + ["ld%d" % k for k in range(8)])
+
+A = AluOpType
+F = ActivationFunctionType
+
+
+def rank_program(g, core, T, topo):
+    rank = T.rank_of(core)
+    if rank is None:
+        return
+    n = len(T.cores)
+    Q = {"v": g.vector, "s": g.scalar, "p": g.tensor, "g": g, "y": g.sync}
+    ops = []
+
+    def op(q, fn, r=(), w=(), x=(), ch=None, inc=1):
+        ops.append({"q": q, "fn": fn, "r": list(r), "w": list(w), "x": list(x), "ch": ch, "inc": inc})
+
+    bank = [T.b0, T.b1, T.b2, T.b3]
+    ACC = 3
+
+    def thr_banks(a, b):
+        return ["t%d" % k for k in range(a // 1024, (b - 1) // 1024 + 1)]
+
+    ld = PAR["load"]
+    for k in range(len(ld) - 1):
+        a, b = ld[k], ld[k + 1]
+        op("y", lambda e, a=a, b=b: e.dma_start(T.raw[:, a:b], T.g0[:, a:b]), w=[("raw", a, b)], ch="ld%d" % k, inc=16)
+
+    op("g", lambda e: e.iota(T.seed[:], [[128, 32], [0, 8]], 0, 1, allow_small_or_imprecise_dtypes=True), w=[("seed", 0, 32)])
+    op("g", lambda e: e.iota(T.dif[:], [[-1, 128]], 0, 1, allow_small_or_imprecise_dtypes=True), w=[("dif", 0, 128)])
+    op("g", lambda e: e.iota(T.ci[:, 0:128], [[-16, 8], [0, 16]], 0, 1), w=[("ci", 0, 128)])
+    op("g", lambda e: e.iota(T.ci[:, 128:272], [[-16, 9], [-1000, 16]], 15000, 1), w=[("ci", 128, 272)])
+    op("g", lambda e: e.iota(T.ci[:, 272:288], [[-1, 16]], 16, 1), w=[("ci", 272, 288)])
+    op("g", lambda e: e.iota(T.Kb[:, 11:21], [[64, 10]], -127, 1, allow_small_or_imprecise_dtypes=True), w=[("Kb", 11, 21)])
+    op("v", lambda e: e.memset(T.sm[:, 0:1], 0.0), w=[("sm", 0, 1)])
+    op("s", lambda e: e.activation(T.wide[:, :, 0:8], T.seed[:], F.Exp, bias=-C * MID, scale=C),
+       r=[("seed", 0, 32)], w=[("wide", 0, 32)])
+    op("s", lambda e: e.activation(T.sm[:, 1:2], T.sm[:, 0:1], F.Exp, bias=-C * MID, scale=C),
+       r=[("sm", 0, 1)], w=[("sm", 1, 2)])
+    op("v", lambda e: e.tensor_scalar(T.X[:, 0:128], T.dif[:], 0.0, None, A.is_equal), r=[("dif", 0, 128)], w=[("X", 0, 128)])
+    op("v", lambda e: e.tensor_scalar(T.X[:, 128:256], T.dif[:], 0.0, -1.0, A.is_equal, A.mult), r=[("dif", 0, 128)], w=[("X", 128, 256)])
+    op("v", lambda e: e.tensor_scalar(T.I128[:], T.dif[:], 0.0, 128.0, A.is_equal, A.mult), r=[("dif", 0, 128)], w=[("I128", 0, 128)])
+    op("v", lambda e: e.tensor_scalar(T.negI[:], T.dif[:], 0.0, -1.0, A.is_equal, A.mult), r=[("dif", 0, 128)], w=[("negI", 0, 128)])
+    op("v", lambda e: e.tensor_scalar(T.cj[:, 0:272], T.ci[:, 0:272], 4, None, A.arith_shift_right), r=[("ci", 0, 272)], w=[("cj", 0, 272)])
+    for c0 in (0, 16):
+        for wd in (8, 16, 32, 64):
+            op("v", lambda e, c0=c0, wd=wd: e.tensor_copy(T.wide[:, c0:c0 + 16, wd:2 * wd], T.wide[:, c0:c0 + 16, 0:wd]),
+               r=[("wide", c0, c0 + 16)], w=[("wide", c0, c0 + 16)])
+        for c in range(c0, c0 + 16):
+            op("p", lambda e, c=c: e.transpose(T.thr[:, 128 * c:128 * c + 128], T.wide[:, c, :], T.X[:, 0:128]),
+               r=[("wide", c, c + 1), ("X", 0, 128)], x=thr_banks(128 * c, 128 * c + 128))
+    op("v", lambda e: e.tensor_scalar(T.cj[:, 272:288], T.ci[:, 272:288], 15, None, A.bitwise_and), r=[("ci", 272, 288)], w=[("cj", 272, 288)])
+    op("v", lambda e: e.tensor_scalar(T.G[:], T.cj[:, 0:128], 0.0, None, A.is_equal), r=[("cj", 0, 128)], w=[("G", 0, 128)])
+    op("v", lambda e: e.tensor_scalar(T.Zoff[:], T.cj[:, 128:272], 0.0, -1.0e9, A.not_equal, A.mult), r=[("cj", 128, 272)], w=[("Zoff", 0, 144)])
+    op("v", lambda e: e.tensor_scalar(T.M16[:], T.cj[:, 272:288], 0.0, None, A.is_equal), r=[("cj", 272, 288)], w=[("M16", 0, 16)])
+
+    st = {"done": 0, "first": True}
+
+    def key_sub(t):
+        if t < 0:
+            op("p", lambda e: e.matmul(bank[ACC][:, 0:1], T.negI[:], T.Kb[:, 11:12], False, False),
+               r=[("Kb", 11, 12), ("negI", 0, 128)], x=["b3"])
+        else:
+            op("p", lambda e: e.matmul(bank[ACC][:, 0:2], T.negI[:], T.Kb[:, t:t + 13:12], False, False),
+               r=[("Kb", t, t + 1), ("Kb", t + 12, t + 13), ("negI", 0, 128)], x=["b3"])
+
+    def add_up(a, b, t):
+        for u in range(a, b, NR):
+            wd = min(NR, b - u)
+            st["done"] += wd
+            first, last = st["first"], st["done"] == W
+            op("p", lambda e, u=u, wd=wd, first=first, last=last:
+               e.matmul(bank[ACC][:, 0:wd], T.I128[:], T.cmp[:, u:u + wd], first, last),
+               r=[("cmp", u, u + wd), ("I128", 0, 128)], x=["b3"])
+            if first:
+                st["first"] = False
+                key_sub(t)
+        if st["done"] == W:
+            st["done"] = 0
+            st["first"] = True
+
+    def compare(src, name, a, b, t):
+        op("v", lambda e: e.tensor_tensor(T.cmp[:, a:b], src[:, a:b], T.thr[:, a:b], A.is_gt),
+           r=[(name, a, b)], w=[("cmp", a, b)], x=thr_banks(a, b))
+        add_up(a, b, t)
+
+    def key0(t):
+        op("v", lambda e: e.tensor_scalar(T.rk[:], T.M16[:], T.Kb[:, t:t + 1], None, A.mult),
+           r=[("M16", 0, 16), ("Kb", t, t + 1)], w=[("rk", 0, 16)])
+
+    def key1():
+        op("p", lambda e: e.matmul(bank[ACC][:, 128:144], T.G[:], T.rk[:], True, True), r=[("G", 0, 128), ("rk", 0, 16)], x=["b3"])
+
+    def key2(t):
+        op("v", lambda e: e.tensor_reduce(T.sm[:, 4:5], bank[ACC][:, 128:144], AxisListType.X, A.max), w=[("sm", 4, 5)], x=["b3"])
+        op("v", lambda e: e.tensor_scalar(T.Z[:], T.Zoff[:], T.Kb[:, t:t + 1], T.sm[:, 4:5], A.add, A.is_ge),
+           r=[("Zoff", 0, 144), ("Kb", t, t + 1), ("sm", 4, 5)], w=[("Z", 0, 144)])
+
+    def elect_mm(k, bi):
+        a, b = PAR["eb"][k], PAR["eb"][k + 1]
+        wd = (b - a) // 16
+        for i in range(16):
+            op("p", lambda e, i=i: e.matmul(bank[bi][:, 256:256 + wd], T.Z[:, 15 - i:143 - i], T.p[:, a + i:b:16], i == 0, i == 15),
+               r=[("Z", 0, 144), ("p", a, b)], x=["b%d" % bi])
+
+    def elect_ln(k, bi):
+        j0, j1 = PAR["eb"][k] // 16, PAR["eb"][k + 1] // 16
+        op("s", lambda e: e.activation(T.lnx[:, j0:j1], bank[bi][:, 256:256 + j1 - j0], F.Ln), w=[("lnx", j0, j1)], x=["b%d" % bi])
+
+    def elect_round(k, rnd):
+        j0, j1 = PAR["eb"][k] // 16, PAR["eb"][k + 1] // 16
+        off = T["off%d" % rnd]
+        op("v", lambda e: e.tensor_scalar(off[:, j0:j1], T.lnx[:, j0:j1], T.sm[:, 2:3], 1.0 / C, A.subtract, A.mult),
+           r=[("lnx", j0, j1), ("sm", 2, 3)], w=[("off%d" % rnd, j0, j1)])
+        if j1 == KB:
+            dst = T.cores[(rank - 1 - rnd % (n - 1)) % n]
+            rid, pid, _ = topo.addr(dst)
+            op("g", lambda e: e.remote_dma(T["land%d" % rnd][:, 0:KB], off[:, 0:KB], T.sem["arr%d" % rnd], T.sem.sent,
+                                           pid, rid, topo.mask(core, dst)),
+               r=[("off%d" % rnd, 0, KB)], ch="sent", inc=len(topo.engines(core, dst)))
+            src = T.cores[(rank + 1 + rnd % (n - 1)) % n]
+            op(None, None, w=[("land%d" % rnd, 0, KB)], ch="arr%d" % rnd, inc=len(topo.engines(src, core)))
+
+    def decide(t, split):
+        op("v", lambda e: e.tensor_reduce(T.sm[:, 8:9], bank[ACC][:, 0:NR], AxisListType.X, A.add), w=[("sm", 8, 9)], x=["b3"])
+        op("v", lambda e: e.tensor_scalar(T.DX[:], T.X[:], T.sm[:, 8:9], 0.0, A.mult, A.is_gt),
+           r=[("X", 0, 256), ("sm", 8, 9)], w=[("DX", 0, 256)])
+        op("v", lambda e: e.tensor_scalar(T.Kb[:, t + 1:t + 2], T.sm[:, 8:9], -64.0, T.Kb[:, t:t + 1], A.max, A.add),
+           r=[("sm", 8, 9), ("Kb", t, t + 1)], w=[("Kb", t + 1, t + 2)])
+        if split:
+            op("v", lambda e: e.tensor_scalar(T.nb[:, 0:1], T.sm[:, 8:9], 0.0, -1.0, A.is_gt, A.mult), r=[("sm", 8, 9)], w=[("nb", 0, 1)])
+            op("v", lambda e: e.tensor_scalar(T.nb[:, 2:3], T.sm[:, 8:9], 0.0, -1.0, A.is_lt, A.mult), r=[("sm", 8, 9)], w=[("nb", 2, 3)])
+
+    def pick(a, b, bi):
+        op("p", lambda e: e.matmul(bank[bi][:, 0:b - a], T.DX[:, 0:128], T.h[:, a:b], True, False),
+           r=[("DX", 0, 128), ("h", a, b)], x=["b%d" % bi])
+        op("p", lambda e: e.matmul(bank[bi][:, 0:b - a], T.DX[:, 128:256], T.p[:, a:b], False, True),
+           r=[("DX", 128, 256), ("p", a, b)], x=["b%d" % bi])
+
+    def phase(plan, oname, rnd, t):
+        for it in plan:
+            k = it[0]
+            if k == "em":
+                elect_mm(it[1], it[2])
+            elif k == "el":
+                elect_ln(it[1], it[2])
+            elif k == "er":
+                elect_round(it[1], rnd)
+            elif k == "k0":
+                key0(t + 1)
+            elif k == "k1":
+                key1()
+            elif k == "k2":
+                key2(t + 1)
+            else:
+                a, b = it[1], it[2]
+                if k in ("gv", "gs", "tg"):
+                    offs = T[oname]
+                    rd = [("p", 0, W), (oname, a // 16, b // 16)]
+                    win = T.p[:, 0:W].indirect(offs[:, a // 16:b // 16])
+                if k == "gv":
+                    op("v", lambda e, a=a, b=b, win=win: e.tensor_copy(T.h[:, a:b], win), r=rd, w=[("h", a, b)])
+                elif k == "gs":
+                    op("s", lambda e, a=a, b=b, win=win: e.activation(T.h[:, a:b], win, F.Copy), r=rd, w=[("h", a, b)])
+                elif k == "tg":
+                    op("v", lambda e, a=a, b=b, win=win: e.tensor_tensor(T.cmp[:, a:b], win, T.ths[:, a:b], A.is_gt),
+                       r=rd + [("ths", a, b)], w=[("cmp", a, b)])
+                    add_up(a, b, t)
+                elif k == "tv":
+                    op("v", lambda e, a=a, b=b: e.tensor_copy(T.ths[:, a:b], T.thr[:, a:b]), w=[("ths", a, b)], x=thr_banks(a, b))
+                elif k == "c":
+                    compare(T.h, "h", a, b, t)
+                elif k == "pe":
+                    bi = it[3]
+                    pick(a, b, bi)
+                    if it[4] == "s":
+                        op("s", lambda e, a=a, b=b, bi=bi: e.activation(T.p[:, a:b], bank[bi][:, 0:b - a], F.Copy),
+                           w=[("p", a, b)], x=["b%d" % bi])
+                    else:
+                        op("v", lambda e, a=a, b=b, bi=bi: e.tensor_copy(T.p[:, a:b], bank[bi][:, 0:b - a]),
+                           w=[("p", a, b)], x=["b%d" % bi])
+                elif k == "va":
+                    op("v", lambda e, a=a, b=b: e.tensor_scalar(T.h[:, a:b], T.h[:, a:b], T.nb[:, 0:1], T.nb[:, 2:3], A.mult, A.add),
+                       r=[("h", a, b), ("nb", 0, 3)], w=[("h", a, b)])
+                elif k == "vb":
+                    op("v", lambda e, a=a, b=b: e.tensor_scalar(T.cmp[:, a:b], T.p[:, a:b], T.nb[:, 2:3], T.nb[:, 0:1], A.mult, A.add),
+                       r=[("p", a, b), ("nb", 0, 3)], w=[("cmp", a, b)])
+                else:
+                    op("v", lambda e, a=a, b=b: e.tensor_tensor_scan(T.p[:, a:b], T.h[:, a:b], T.cmp[:, a:b], 1.0, A.min, A.mult),
+                       r=[("cmp", a, b), ("h", a, b)], w=[("p", a, b)])
+
+    sub = PAR["sub"]
+    for k in range(len(sub) - 1):
+        a, b = sub[k], sub[k + 1]
+        op("s", lambda e, a=a, b=b: e.activation(T.p[:, a:b], T.raw[:, a:b], F.Exp, bias=-C * MID, scale=C),
+           r=[("raw", a, b)], w=[("p", a, b)])
+        compare(T.p, "p", a, b, -1)
+    op("s", lambda e: e.activation(T.sm[:, 2:3], T.sm[:, 1:2], F.Ln), r=[("sm", 1, 2)], w=[("sm", 2, 3)])
+    op("v", lambda e: e.tensor_reduce(T.Kb[:, 0:1], bank[ACC][:, 0:NR], AxisListType.X, A.add), w=[("Kb", 0, 1)], x=["b3"])
+    key0(0)
+    key1()
+    key2(0)
+    phase(PAR["e0"], None, 0, -1)
+
+    for rnd in range(RO):
+        t = 2 * rnd
+        phase(PAR["g0"], "off%d" % rnd, rnd, t)
+        decide(t, True)
+        phase(PAR["s0"], None, rnd, t)
+        phase(PAR["g1"], "land%d" % rnd, rnd, t + 1)
+        decide(t + 1, rnd < RO - 1)
+        if rnd < RO - 1:
+            phase(PAR["s1"], None, rnd + 1, t + 1)
+
+    fin = PAR["fin"]
+    lo = [0]
+
+    def finish(a, b, eng):
+        if eng == "s":
+            op("s", lambda e: e.activation(T.lin[:, a:b], T.lin[:, a:b], F.Identity, bias=MAGIC + MID, scale=1.0 / C),
+               r=[("lin", a, b)], w=[("lin", a, b)])
+        else:
+            op("v", lambda e: e.tensor_scalar(T.lin[:, a:b], T.lin[:, a:b], 1.0 / C, MAGIC + MID, A.mult, A.add),
+               r=[("lin", a, b)], w=[("lin", a, b)])
+        op("v", lambda e: e.tensor_scalar(T.lin[:, a:b], T.lin[:, a:b], -MAGIC, None, A.add), r=[("lin", a, b)], w=[("lin", a, b)])
+        if b in PAR["store"]:
+            a3 = lo[0]
+            lo[0] = b
+            op("y", lambda e: e.dma_start(T.yg[:, a3:b], T.lin[:, a3:b]), r=[("lin", a3, b)], ch="stored", inc=16)
+
+    held = []
+    for k in range(len(fin)):
+        a, b, eng = fin[k]
+        bi = k % 4
+        pick(a, b, bi)
+        op("s", lambda e, a=a, b=b, bi=bi: e.activation(T.lin[:, a:b], bank[bi][:, 0:b - a], F.Ln), w=[("lin", a, b)], x=["b%d" % bi])
+        if held:
+            finish(*held.pop())
+        if eng == "s" and k < len(fin) - 1:
+            held.append(fin[k])
+        else:
+            finish(a, b, eng)
+        if k == 0:
+            op("v", lambda e: e.tensor_scalar(T.ec[:, 0:1], T.Kb[:, 2 * RO:2 * RO + 1], T.Kb[:, 19:20], -1.0 / 128, A.add, A.mult),
+               r=[("Kb", 2 * RO, 2 * RO + 1), ("Kb", 19, 20)], w=[("ec", 0, 1)])
+        if k == PAR["yek"]:
+            op("p", lambda e: e.matmul(bank[ACC][0:1, 0:128], T.ec[:, 0:1], T.negI[:], True, True),
+               r=[("ec", 0, 1), ("negI", 0, 128)], x=["b3"])
+            op("v", lambda e: e.tensor_copy(T.dif[0:1, :], bank[ACC][0:1, 0:128]), w=[("dif", 0, 128)], x=["b3"])
+            op("y", lambda e: e.dma_start(T.ye[:], T.dif[0:1, :]), r=[("dif", 0, 128)], ch="stored", inc=16)
+
+    def meet(u, v):
+        for (n1, a1, b1) in u:
+            for (n2, a2, b2) in v:
+                if n1 == n2 and a1 < b2 and a2 < b1:
+                    return True
+        return False
+
+    known = {q: {} for q in Q}
+    by_ch = {}
+    clock = []
+    waits = []
+    marked = set()
+    for i, o in enumerate(ops):
+        q = o["q"]
+        own = o["ch"] or q
+        if q is None:
+            clock.append({own: i})
+            waits.append([])
+            by_ch.setdefault(own, []).append(i)
+            continue
+        need = []
+        for ch, lst in by_ch.items():
+            same = o["ch"] is None and ch == q
+            if same and q == "p":
+                continue
+            for j in reversed(lst):
+                if known[q].get(ch, -1) >= j:
+                    break
+                e = ops[j]
+                hit = meet(e["w"], o["r"]) or meet(e["w"], o["w"]) or meet(e["r"], o["w"])
+                if hit or (not same and len(set(e["x"]) & set(o["x"])) > 0):
+                    need.append(j)
+                    break
+        ws = []
+        for j in sorted(need, reverse=True):
+            if known[q].get(ops[j]["ch"] or ops[j]["q"], -1) >= j:
+                continue
+            ws.append(j)
+            marked.add(j)
+            for c2, j2 in clock[j].items():
+                if known[q].get(c2, -1) < j2:
+                    known[q][c2] = j2
+        waits.append(ws)
+        ck = dict(known[q])
+        ck[own] = i
+        clock.append(ck)
+        by_ch.setdefault(own, []).append(i)
+
+    semof = {"v": "cv", "s": "cs", "p": "cp", "g": "cg"}
+    total = {}
+    count = {}
+    for i, o in enumerate(ops):
+        if o["ch"] is not None or i in marked:
+            name = o["ch"] or semof[o["q"]]
+            total[name] = total.get(name, 0) + o["inc"]
+            count[i] = (name, total[name])
+    for i, o in enumerate(ops):
+        if o["q"] is None:
+            continue
+        e = Q[o["q"]]
+        for j in waits[i]:
+            e.wait_ge(T.sem[count[j][0]], count[j][1])
+        ins = o["fn"](e)
+        if i in count and o["ch"] != "sent":
+            ins.then_inc(T.sem[count[i][0]], o["inc"])
+    g.wait_ge(T.sem.sent, total["sent"])
+    g.sync.wait_ge(T.sem.stored, total["stored"])

@@ -1,68 +1,140 @@
+import math
 from concourse.mybir import AluOpType, AxisListType, ActivationFunctionType
 
 W = 4032
+WP = 4096
 RO = 4
 KB = W // 16
-C = 0.021
+C = math.log(2.0) / 64
 MID = 2016.0
+ENC = C * (0.0225 - MID)
 MAGIC = 12582912.0
-NR = 96
+BIG = 2.0 ** 76
 
 PAR = {
-    "load": [0, 1888, 3040, 3744, 4032],
-    "sub": [0, 608, 1248, 1888, 2464, 3040, 3392, 3744, 4032],
-    "eb": [0, 1184, 2464, 4032],
-    "e0": [("em", 0, 3), ("tv", 0, 640), ("tv", 3168, 4032), ("el", 0, 3), ("er", 0)],
-    "g0": [("em", 1, 0), ("em", 2, 1), ("tg", 0, 640), ("gs", 640, 1184), ("el", 1, 0), ("er", 1), ("gs", 1728, 2464),
-           ("c", 640, 1184), ("gv", 1184, 1728), ("el", 2, 1), ("er", 2), ("c", 1184, 2464), ("gs", 2464, 3200),
-           ("c", 2464, 3200), ("gs", 3200, 3680), ("c", 3200, 3680), ("gs", 3680, 3936), ("c", 3680, 3936),
-           ("gs", 3936, 4032), ("c", 3936, 4032), ("gs", 0, 640)],
-    "g1": [("tg", 3168, 4032), ("gv", 0, 224), ("c", 0, 224), ("gs", 224, 1472), ("c", 224, 1472), ("gs", 1472, 2272),
-           ("c", 1472, 2272), ("gs", 2272, 2784), ("c", 2272, 2784), ("gs", 2784, 3072), ("c", 2784, 3072),
-           ("gs", 3072, 3168), ("c", 3072, 3168), ("gs", 3168, 4032)],
-    "s0": [("pe", 1568, 1888, 0, "s"), ("vb", 0, 1568), ("va", 0, 1568), ("vc", 0, 1568), ("pe", 1888, 2336, 1, "s"),
-           ("pe", 2336, 2816, 2, "s"), ("pe", 2816, 3264, 3, "s"), ("pe", 3264, 3744, 0, "s"), ("pe", 3744, 4032, 1, "v")],
-    "s1": [("k0",), ("pe", 0, 416, 0, "s"), ("pe", 416, 800, 1, "s"), ("k1",), ("vb", 2176, 4032), ("k2",),
-           ("va", 2176, 4032), ("vc", 2176, 4032), ("pe", 800, 1216, 2, "s"), ("pe", 1216, 1632, 0, "s"),
-           ("pe", 1632, 2048, 1, "s"), ("em", 0, 3), ("el", 0, 3), ("pe", 2048, 2176, 2, "s"), ("er", 0)],
-    "fin": [(0, 256, "v"), (256, 704, "v"), (704, 1184, "v"), (1184, 1664, "s"), (1664, 2112, "v"), (2112, 2592, "s"),
-            (2592, 3072, "s"), (3072, 3552, "s"), (3552, 4032, "s")],
-    "store": [256, 704, 1184, 2112, 3072, 4032],
+    "sets": [[(8 + i, 12 + i) for i in range(4)] + [(16 + i, 24 + i) for i in range(8)],
+             [(12 + i, i) for i in range(12)]],
+    "stages": [[0, 4, 8, 10, 12], [0, 4, 8, 10, 12]],
+    "direct": [(0, 1024), (3072, 4032)],
+    "load": [0, 1920, 3072, 3840, 4032],
+    "sub": [0, 640, 1280, 1920, 2560, 3072, 3456, 3840, 4032],
+    "eb": [0, 1024, 2048, 4032],
+    "e0": [("em", 0, 4), ("em", 1, 3), ("el", 0, 4), ("er", 0), ("el", 1, 3), ("er", 1)],
+    "g0": [("em", 2, 4), ("tg", 0, 1024), ("gs", 1024, 1536), ("z",), ("gs", 1536, 2048), ("t", 0, 0, 4), ("el", 2, 4), ("er", 2),
+           ("t", 1, 0, 4), ("m", 0, 1024, 3), ("gs", 2048, 2560), ("c", 0, 4), ("r", 3), ("gv", 2816, 3072), ("gs", 3072, 3584), ("t", 0, 4, 8), ("n", 0, 4),
+           ("j",), ("t", 1, 4, 8), ("gs", 2560, 2816), ("c", 4, 8), ("gs", 3584, 3840), ("t", 0, 8, 10), ("t", 1, 8, 10), ("gs", 3840, 4032),
+           ("n", 4, 8), ("c", 8, 10), ("t", 0, 10, 12), ("t", 1, 10, 12), ("gs", 0, 1024), ("n", 8, 10), ("c", 10, 12), ("pf", 1536, 2048, 0),
+           ("n", 10, 12)],
+    "s0": [("d",), ("nb",), ("u",), ("pk", 1536, 2048, 0), ("cs", 1536, 2048, 0), ("pf", 2048, 2560, 1), ("pk", 2048, 2560, 1),
+           ("vb", 0, 1536), ("cs", 2048, 2560, 1), ("pf", 2560, 3072, 2), ("pk", 2560, 3072, 2), ("va", 0, 1536), ("cs", 2560, 3072, 2),
+           ("pf", 3072, 3584, 3), ("pk", 3072, 3584, 3), ("cs", 3072, 3584, 3), ("pf", 3584, 4032, 4), ("pk", 3584, 4032, 4),
+           ("vc", 0, 1536), ("cs", 3584, 4032, 4), ("k",)],
+    "g1": [("tg", 3072, 4032), ("gs", 0, 512), ("z",), ("gs", 1536, 2048), ("t", 1, 0, 4), ("m", 3072, 4032, 3), ("gv", 1280, 1536),
+           ("t", 0, 0, 4), ("gs", 512, 1024), ("c", 0, 4), ("r", 3), ("pf", 0, 512, 0), ("gs", 2048, 2560), ("t", 1, 4, 8), ("n", 0, 4), ("j",),
+           ("t", 0, 4, 8), ("gs", 1024, 1280), ("c", 4, 8), ("gs", 2560, 2816), ("t", 1, 8, 10), ("pf", 512, 1024, 1), ("t", 0, 8, 10), ("gs", 2816, 3072),
+           ("n", 4, 8), ("c", 8, 10), ("t", 1, 10, 12), ("t", 0, 10, 12), ("gs", 3072, 4032), ("n", 8, 10), ("c", 10, 12), ("pf", 1024, 1536, 2),
+           ("n", 10, 12)],
+    "s1": [("d",), ("u",), ("k",), ("pk", 0, 512, 0), ("k0",), ("pk", 512, 1024, 1), ("nb",), ("cs", 0, 512, 0), ("k1",),
+           ("vb", 2560, 4032), ("pk", 1024, 1536, 2), ("cs", 512, 1024, 1), ("pf", 1536, 2048, 3), ("pk", 1536, 2048, 3), ("k2",),
+           ("cs", 1024, 1536, 2), ("pf", 2048, 2560, 4), ("pk", 2048, 2560, 4), ("cs", 1536, 2048, 3), ("va", 2560, 4032), ("em", 0, 0),
+           ("cs", 2048, 2560, 4), ("el", 0, 0), ("em", 1, 1), ("vc", 2560, 4032), ("el", 1, 1), ("er", 0), ("er", 1)],
+    "fin": [(0, 256, "v"), (256, 512, "v"), (512, 1024, "v"), (1024, 1536, "s"), (1536, 2048, "v"), (2048, 2560, "s"),
+            (2560, 3072, "s"), (3072, 3584, "s"), (3584, 4032, "s")],
+    "store": [256, 512, 1024, 2048, 3072, 4032],
     "yek": 7,
 }
+PAR.update({
+    "g0": [("em", 2, 4), ("gs", 1024, 1536), ("tg", 0, 1024), ("t", 0, 0, 4), ("z",), ("el", 2, 4), ("er", 2), ("gv", 3072, 3584),
+           ("m", 0, 1024, 3), ("gs", 1536, 2048), ("r", 3), ("t", 1, 0, 4), ("gs", 2048, 2560), ("t", 0, 4, 8), ("t", 1, 4, 8), ("c", 0, 4),
+           ("n", 0, 4), ("gs", 2560, 2816), ("t", 0, 8, 10), ("gs", 3584, 3840), ("t", 1, 8, 10), ("j",), ("c", 4, 8), ("n", 4, 8),
+           ("gs", 2816, 3072), ("t", 0, 10, 12), ("gs", 3840, 4032), ("t", 1, 10, 12), ("pf", 1536, 2048, 0), ("c", 8, 10), ("n", 8, 10),
+           ("gs", 0, 1024), ("c", 10, 12), ("n", 10, 12)],
+    "s0": [("d",), ("pk", 1536, 2048, 0), ("pf", 2048, 2560, 1), ("u",), ("us",), ("nb",), ("vb", 0, 1536), ("pk", 2048, 2560, 1),
+           ("cs", 1536, 2048, 0), ("pf", 2560, 3072, 2), ("cs", 2048, 2560, 1), ("va", 0, 1536), ("pk", 2560, 3072, 2), ("k",),
+           ("pf", 3072, 3584, 3), ("pk", 3072, 3584, 3), ("pf", 3840, 4032, 0), ("vc", 0, 1536), ("cs", 2560, 3072, 2),
+           ("pk", 3840, 4032, 0), ("cs", 3072, 3584, 3), ("pf", 3584, 3840, 4), ("pk", 3584, 3840, 4), ("cv", 3840, 4032, 0),
+           ("cs", 3584, 3840, 4)],
+    "g1": [("gv", 0, 512), ("z",), ("t", 1, 0, 4), ("pf", 0, 512, 0), ("gs", 1536, 2048), ("t", 0, 0, 4), ("gs", 512, 1024),
+           ("tg", 3072, 4032), ("t", 1, 4, 8), ("gs", 2048, 2560), ("m", 3072, 4032, 3), ("gs", 1024, 1536), ("c", 0, 4), ("r", 3),
+           ("t", 0, 4, 8), ("t", 1, 8, 10), ("n", 0, 4), ("c", 4, 8), ("gs", 2560, 2816), ("gs", 3072, 4032), ("t", 0, 8, 10),
+           ("t", 1, 10, 12), ("j",), ("gv", 2816, 3072), ("n", 4, 8), ("t", 0, 10, 12), ("pf", 512, 1024, 1), ("c", 8, 10), ("c", 10, 12),
+           ("n", 8, 10), ("n", 10, 12), ("pf", 1024, 1536, 2)],
+    "s1": [("d",), ("u",), ("us",), ("pk", 0, 512, 0), ("cs", 0, 512, 0), ("pf", 1536, 2048, 3), ("nb",), ("pk", 512, 1024, 1), ("k",), ("k0",),
+           ("k1",), ("pk", 1024, 1536, 2), ("vb", 2560, 4032), ("k2",), ("cs", 512, 1024, 1), ("cs", 1024, 1536, 2),
+           ("pf", 2048, 2560, 4), ("pk", 1536, 2048, 3), ("pk", 2048, 2560, 4), ("cs", 1536, 2048, 3), ("va", 2560, 4032), ("em", 0, 0),
+           ("em", 1, 1), ("vc", 2560, 4032), ("cs", 2048, 2560, 4), ("el", 0, 0), ("el", 1, 1), ("er", 0), ("er", 1)],
+})
+
+
+def last_plan(cuts, scalar_rounds, stores):
+    plan = [("pf", cuts[0], cuts[1], 0), ("d",), ("u",), ("us",), ("k",), ("y0",)]
+    held, lo = [], 0
+    for k in range(len(cuts) - 1):
+        a, b = cuts[k], cuts[k + 1]
+        plan += [("pf", a, b, k % 5)] * (k > 0) + [("pk", a, b, k % 5), ("ln", a, b, k % 5)]
+        ready, held = held, []
+        if k in scalar_rounds and b < W:
+            held = [k]
+        else:
+            ready = ready + [k]
+        for j in ready:
+            plan += [("rs" if j in scalar_rounds else "rv", cuts[j], cuts[j + 1]), ("sv", cuts[j], cuts[j + 1])]
+            if cuts[j + 1] in stores:
+                plan.append(("st", lo, cuts[j + 1]))
+                lo = cuts[j + 1]
+        plan += [("y1",), ("y2",)] * (k == 3)
+    return plan
+
+
+PAR.update({
+    "sets": [[(i, 8 + i) for i in range(8)] + [(20 + i, 16 + i) for i in range(4)],
+             [(16 + i, i) for i in range(8)] + [(24 + i, 28 + i) for i in range(4)]],
+    "direct": [(3072, 4032), (1024, 2048)],
+    "eb": [0, 2048, 4032], "mw": 64,
+    "e0": [("em", 0, 4), ("ev", 0, 4), ("et", 0, 4), ("el", 0, 4), ("er", 0)],
+'g0': [('em',1,0),('gv',0,320),('ev',1,0),('et',1,0),('gv',320,768),('gs',1024,1664),('el',1,0),('gs',1664,2048),('er',1),('t',0,0,2),('gs',768,1024),('t',1,0,2),('gs',2048,2560),('t',0,2,3),('t',0,3,6),('t',1,2,6),('c',0,2),('t',1,6,8),('gs',2560,2816),('tg',3072,3584),('n',0,1),('gs',2816,3072),('t',0,6,8),('c',2,8),('m',3072,3520,2),('tg',3584,3968),('n',1,6),('t',1,10,12),('t',1,8,10),('t',0,8,10),('m',3520,3584,2),('t',0,10,12),('m',3584,3968,2),('tg',3968,4032),('m',3968,4032,2),('c',8,11),('r',2),('gs',3072,4032),('c',11,12),('n',6,10),('j',),('n',10,12)],
+'s0': [('d',),('pf',0,512,0),('u',),('pk',0,512,0),('pf',512,1024,1),('us',),('pk',512,1024,1),('pf',1024,1536,2),('pk',1024,1536,2),('nb',),('k',),('pf',1536,2048,4),('vb',2560,4032),('cs',0,512,0),('cs',512,1024,1),('pk',1536,2048,4),('va',2560,2880),('cs',1024,1536,2),('pf',2176,2560,3),('va',2880,4032),('pk',2176,2560,3),('cs',1536,2048,4),('pf',2048,2176,2),('vc',2560,2880),('pk',2048,2176,2),('vc',2880,4032),('cv',2176,2560,3),('cs',2048,2176,2)],
+'g1': [('gs',2048,2592),('t',0,0,4),('gv',0,672),('t',1,0,4),('gs',672,1024),('tg',1024,1536),('gs',2592,3136),('t',1,4,8),('m',1024,1536,1),('t',0,4,8),('tg',1536,2048),('m',1536,2048,1),('gs',3136,3584),('gs',3584,3840),('c',0,8),('n',0,3),('t',0,8,10),('n',3,6),('t',1,8,10),('r',1),('t',0,10,12),('gs',3840,4032),('gs',1024,1952),('t',1,10,12),('j',),('c',8,12),('n',6,12),('pf',512,1024,2),('gv',1952,2048),('pf',2816,3072,4)],
+'s1': [('nb',),('pf',0,512,3),('u',),('us',),('d',),('pk',0,512,3),('k',),('vb',1024,2048),('pk',512,1024,2),('k0',),('k1',),('pf',3584,4032,1),('va',1024,2048),('pk',3584,4032,1),('cs',0,512,3),('pf',3072,3584,0),('pk',3072,3584,0),('k2',),('vc',1024,2048),('vb',2048,2816),('cs',512,1024,2),('em',0,2),('va',2048,2816),('pk',2816,3072,4),('cs',3584,4032,1),('ev',0,2),('cs',3072,3584,0),('vc',2048,2816),('et',0,2),('cs',2816,3072,4),('el',0,2),('er',0)],
+'stages': [[0,2,6,10,12],[0,4,8,10,12]],
+    "fin": last_plan([0, 160, 512, 1024, 1504, 1696, 2048, 2560, 3072, 3584, 3840, 4032], (3, 4, 7, 8, 9, 10), (160, 512, 1024, 2048, 3072, 4032)),
+})
+FOOT = {}
 
 SCRATCH = {
     "raw": ("sbuf", [128, W], "int32"),
     "lin": ("sbuf", [128, W], "float32"),
-    "p": ("sbuf", [128, W], "bfloat16"),
-    "h": ("sbuf", [128, W], "bfloat16"),
-    "cmp": ("sbuf", [128, W], "bfloat16"),
+    "p": ("sbuf", [128, WP], "bfloat16"),
+    "h": ("sbuf", [128, WP], "bfloat16"),
+    "cm": ("sbuf", [128, WP], "bfloat16"),
+    "fb": ("sbuf", [128, WP], "bfloat16"),
     "ths": ("sbuf", [128, W], "bfloat16"),
-    "seed": ("sbuf", [128, 32, 8], "float32"),
-    "wide": ("sbuf", [128, 32, 128], "bfloat16"),
+    "th": ("sbuf", [128, 32], "bfloat16"),
+    "nb": ("sbuf", [128, 4], "bfloat16"),
     "dif": ("sbuf", [128, 128], "float32"),
-    "ci": ("sbuf", [128, 288], "int32"),
-    "cj": ("sbuf", [128, 288], "int32"),
-    "X": ("sbuf", [128, 256], "bfloat16"),
-    "DX": ("sbuf", [128, 256], "bfloat16"),
-    "I128": ("sbuf", [128, 128], "bfloat16"),
+    "ci": ("sbuf", [128, 144], "int32"),
+    "cj": ("sbuf", [128, 144], "int32"),
+    "I": ("sbuf", [128, 1024], "bfloat16"),
+    "X": ("sbuf", [128, 128], "bfloat16"),
+    "D": ("sbuf", [128, 128], "bfloat16"),
     "negI": ("sbuf", [128, 128], "float32"),
     "G": ("sbuf", [128, 128], "float32"),
     "M16": ("sbuf", [128, 16], "float32"),
     "rk": ("sbuf", [128, 16], "float32"),
-    "Zoff": ("sbuf", [128, 144], "bfloat16"),
-    "Z": ("sbuf", [128, 144], "bfloat16"),
-    "Kb": ("sbuf", [128, 24], "float32"),
+    "Zoff": ("sbuf", [128, 8], "bfloat16"),
+    "Z": ("sbuf", [128, 8], "bfloat16"),
+    "es": ("sbuf", [128, 256], "bfloat16"),
+    "run": ("sbuf", [128, 256], "float32"),
+    "Kb": ("sbuf", [128, 16], "float32"),
+    "cb": ("sbuf", [128, 4], "bfloat16"),
     "sm": ("sbuf", [128, 16], "float32"),
-    "nb": ("sbuf", [128, 16], "bfloat16"),
     "ec": ("sbuf", [128, 4], "float32"),
     "lnx": ("sbuf", [128, 256], "float32"),
-    "thr": ("psum", [128, 4096], "bfloat16"),
-    "b0": ("psum", [128, 512], "float32"),
-    "b1": ("psum", [128, 512], "float32"),
-    "b2": ("psum", [128, 512], "float32"),
-    "b3": ("psum", [128, 512], "float32"),
+    "t0": ("psum", [128, 1024], "bfloat16"),
+    "t1": ("psum", [128, 1024], "bfloat16"),
 }
+for _b in range(6):
+    SCRATCH["b%d" % _b] = ("psum", [128, 512], "float32")
 for _t in range(RO):
     SCRATCH["off%d" % _t] = ("sbuf", [128, 256], "uint16")
     SCRATCH["land%d" % _t] = ("sbuf", [128, 256], "uint16")
@@ -74,6 +146,19 @@ A = AluOpType
 F = ActivationFunctionType
 
 
+def shift_of(step, a):
+    for s in PAR["sets"][step]:
+        if a // 128 in s:
+            return 2 * (a // 128 - s[0])
+    return 0
+
+
+def slot_of(step, i):
+    sets, stages = PAR["sets"][step], PAR["stages"][step]
+    k = max(k for k in range(len(stages)) if stages[k] <= i)
+    return k % 2, sum(len(s) for s in sets[stages[k]:i]), 128 * sum(len(s) for s in sets[:i])
+
+
 def rank_program(g, core, T, topo):
     rank = T.rank_of(core)
     if rank is None:
@@ -83,99 +168,119 @@ def rank_program(g, core, T, topo):
     ops = []
 
     def op(q, fn, r=(), w=(), x=(), ch=None, inc=1):
-        ops.append({"q": q, "fn": fn, "r": list(r), "w": list(w), "x": list(x), "ch": ch, "inc": inc})
+        ops.append({"q": q, "fn": fn, "r": list(r), "w": list(w), "x": list(x), "ch": ch, "inc": inc, "tag": FOOT.get("tag")})
 
-    bank = [T.b0, T.b1, T.b2, T.b3]
-    ACC = 3
-
-    def thr_banks(a, b):
-        return ["t%d" % k for k in range(a // 1024, (b - 1) // 1024 + 1)]
+    bank = [T["b%d" % k] for k in range(6)]
+    turn = [T.t0, T.t1]
+    ACC = 5
+    acc = bank[ACC][:, 0:1]
+    XA = ["b%d" % ACC]
+    unit = T.sm[:, 8:9]
+    unit2 = T.nb[:, 0:1]
+    nkeep = T.nb[:, 2:3]
+    shifts = sorted(set(shift_of(s, a) for s in (0, 1) for a in range(0, W, 128)))
+    mw = PAR["mw"]
+    mults = [1.0, -128.0] + [-2.0 ** sh for sh in shifts]
 
     ld = PAR["load"]
     for k in range(len(ld) - 1):
         a, b = ld[k], ld[k + 1]
         op("y", lambda e, a=a, b=b: e.dma_start(T.raw[:, a:b], T.g0[:, a:b]), w=[("raw", a, b)], ch="ld%d" % k, inc=16)
 
-    op("g", lambda e: e.iota(T.seed[:], [[128, 32], [0, 8]], 0, 1, allow_small_or_imprecise_dtypes=True), w=[("seed", 0, 32)])
-    op("g", lambda e: e.iota(T.dif[:], [[-1, 128]], 0, 1, allow_small_or_imprecise_dtypes=True), w=[("dif", 0, 128)])
+    def count_up(out, name, a, b, pattern, base, by):
+        op("g", lambda e: e.iota(out, pattern, base, by, allow_small_or_imprecise_dtypes=True), w=[(name, a, b)])
+
+    count_up(T.lnx[:, 0:32], "lnx", 0, 32, [[128, 32]], 0, 1)
+    count_up(T.dif[:], "dif", 0, 128, [[-1, 128]], 0, 1)
+    count_up(T.cb[:, 2:3], "cb", 2, 3, [[0, 1]], 127, -1)
     op("g", lambda e: e.iota(T.ci[:, 0:128], [[-16, 8], [0, 16]], 0, 1), w=[("ci", 0, 128)])
-    op("g", lambda e: e.iota(T.ci[:, 128:272], [[-16, 9], [-1000, 16]], 15000, 1), w=[("ci", 128, 272)])
-    op("g", lambda e: e.iota(T.ci[:, 272:288], [[-1, 16]], 16, 1), w=[("ci", 272, 288)])
-    op("g", lambda e: e.iota(T.Kb[:, 11:21], [[64, 10]], -127, 1, allow_small_or_imprecise_dtypes=True), w=[("Kb", 11, 21)])
+    op("g", lambda e: e.iota(T.ci[:, 128:144], [[-1, 16]], 16, 1), w=[("ci", 128, 144)])
     op("v", lambda e: e.memset(T.sm[:, 0:1], 0.0), w=[("sm", 0, 1)])
-    op("s", lambda e: e.activation(T.wide[:, :, 0:8], T.seed[:], F.Exp, bias=-C * MID, scale=C),
-       r=[("seed", 0, 32)], w=[("wide", 0, 32)])
+    op("s", lambda e: e.activation(T.th[:], T.lnx[:, 0:32], F.Exp, bias=ENC, scale=C), r=[("lnx", 0, 32)], w=[("th", 0, 32)])
     op("s", lambda e: e.activation(T.sm[:, 1:2], T.sm[:, 0:1], F.Exp, bias=-C * MID, scale=C),
        r=[("sm", 0, 1)], w=[("sm", 1, 2)])
-    op("v", lambda e: e.tensor_scalar(T.X[:, 0:128], T.dif[:], 0.0, None, A.is_equal), r=[("dif", 0, 128)], w=[("X", 0, 128)])
-    op("v", lambda e: e.tensor_scalar(T.X[:, 128:256], T.dif[:], 0.0, -1.0, A.is_equal, A.mult), r=[("dif", 0, 128)], w=[("X", 128, 256)])
-    op("v", lambda e: e.tensor_scalar(T.I128[:], T.dif[:], 0.0, 128.0, A.is_equal, A.mult), r=[("dif", 0, 128)], w=[("I128", 0, 128)])
+    (a0, b0), (a1, b1) = sorted(PAR["direct"])
+    count_up(T.lnx[:, 64:128], "lnx", 64, 128, [[1, 64]], a0, 0)
+    op("s", lambda e: e.activation(T.ths[:, a0:a0 + 64], T.lnx[:, 64:128], F.Exp, bias=ENC, scale=C), r=[("lnx", 64, 128)], w=[("ths", a0, a0 + 64)])
+
+    def octaves(a, b, back):
+        op("v", lambda e: e.tensor_scalar(T.ths[:, a:b], T.ths[:, a - back:b - back], 2.0 ** (back // 64), None, A.mult),
+           r=[("ths", a - back, b - back)], w=[("ths", a, b)])
+
+    def more_codes():
+        wd = 64
+        while a0 + wd < b0:
+            octaves(a0 + wd, min(b0, a0 + 2 * wd), wd)
+            wd *= 2
+        octaves(a1, b1, a1 - a0)
+
+    op("v", lambda e: e.memset(T.p[:, W:WP], 0.0), w=[("p", W, WP)])
+    op("v", lambda e: e.memset(T.h[:, W:WP], 0.0), w=[("h", W, WP)])
+    op("v", lambda e: e.memset(T.cb[:, 0:1], 128.0), w=[("cb", 0, 1)])
+    for j, val in enumerate(mults):
+        op("v", lambda e, j=j, val=val: e.tensor_scalar(T.I[:, 128 * j:128 * j + 128], T.dif[:], 0.0, val, A.is_equal, A.mult),
+           r=[("dif", 0, 128)], w=[("I", 128 * j, 128 * j + 128)])
+    op("v", lambda e: e.tensor_scalar(T.X[:], T.dif[:], 0.0, -1.0e9, A.not_equal, A.mult), r=[("dif", 0, 128)], w=[("X", 0, 128)])
     op("v", lambda e: e.tensor_scalar(T.negI[:], T.dif[:], 0.0, -1.0, A.is_equal, A.mult), r=[("dif", 0, 128)], w=[("negI", 0, 128)])
-    op("v", lambda e: e.tensor_scalar(T.cj[:, 0:272], T.ci[:, 0:272], 4, None, A.arith_shift_right), r=[("ci", 0, 272)], w=[("cj", 0, 272)])
-    for c0 in (0, 16):
-        for wd in (8, 16, 32, 64):
-            op("v", lambda e, c0=c0, wd=wd: e.tensor_copy(T.wide[:, c0:c0 + 16, wd:2 * wd], T.wide[:, c0:c0 + 16, 0:wd]),
-               r=[("wide", c0, c0 + 16)], w=[("wide", c0, c0 + 16)])
-        for c in range(c0, c0 + 16):
-            op("p", lambda e, c=c: e.transpose(T.thr[:, 128 * c:128 * c + 128], T.wide[:, c, :], T.X[:, 0:128]),
-               r=[("wide", c, c + 1), ("X", 0, 128)], x=thr_banks(128 * c, 128 * c + 128))
-    op("v", lambda e: e.tensor_scalar(T.cj[:, 272:288], T.ci[:, 272:288], 15, None, A.bitwise_and), r=[("ci", 272, 288)], w=[("cj", 272, 288)])
+    op("v", lambda e: e.tensor_scalar(T.cj[:, 0:128], T.ci[:, 0:128], 4, None, A.arith_shift_right), r=[("ci", 0, 128)], w=[("cj", 0, 128)])
+    op("v", lambda e: e.tensor_scalar(T.cj[:, 128:144], T.ci[:, 128:144], 15, None, A.bitwise_and), r=[("ci", 128, 144)], w=[("cj", 128, 144)])
     op("v", lambda e: e.tensor_scalar(T.G[:], T.cj[:, 0:128], 0.0, None, A.is_equal), r=[("cj", 0, 128)], w=[("G", 0, 128)])
-    op("v", lambda e: e.tensor_scalar(T.Zoff[:], T.cj[:, 128:272], 0.0, -1.0e9, A.not_equal, A.mult), r=[("cj", 128, 272)], w=[("Zoff", 0, 144)])
-    op("v", lambda e: e.tensor_scalar(T.M16[:], T.cj[:, 272:288], 0.0, None, A.is_equal), r=[("cj", 272, 288)], w=[("M16", 0, 16)])
+    op("v", lambda e: e.tensor_scalar(T.Zoff[:], T.cj[:, 0:128:16], 0.0, -1.0e9, A.not_equal, A.mult), r=[("cj", 0, 128)], w=[("Zoff", 0, 8)])
+    op("v", lambda e: e.tensor_scalar(T.M16[:], T.cj[:, 128:144], 0.0, None, A.is_equal), r=[("cj", 128, 144)], w=[("M16", 0, 16)])
+    op("v", lambda e: e.memset(T.run[:, 129:256], 0.0), w=[("run", 129, 256)])
+    op("v", lambda e: e.tensor_scalar(T.run[:, 128:129], T.cb[:, 2:3], -1.0, None, A.mult), r=[("cb", 2, 3)], w=[("run", 128, 129)])
+    more_codes()
 
-    st = {"done": 0, "first": True}
+    st = {"done": 0, "all": 33}
 
-    def key_sub(t):
-        if t < 0:
-            op("p", lambda e: e.matmul(bank[ACC][:, 0:1], T.negI[:], T.Kb[:, 11:12], False, False),
-               r=[("Kb", 11, 12), ("negI", 0, 128)], x=["b3"])
-        else:
-            op("p", lambda e: e.matmul(bank[ACC][:, 0:2], T.negI[:], T.Kb[:, t:t + 13:12], False, False),
-               r=[("Kb", t, t + 1), ("Kb", t + 12, t + 13), ("negI", 0, 128)], x=["b3"])
+    def into_sum(lhs, rhs, reads):
+        st["done"] += 1
+        first, last = st["done"] == 1, st["done"] == st["all"]
+        op("p", lambda e: e.matmul(acc, lhs, rhs, first, last), r=reads, x=XA)
 
-    def add_up(a, b, t):
-        for u in range(a, b, NR):
-            wd = min(NR, b - u)
-            st["done"] += wd
-            first, last = st["first"], st["done"] == W
-            op("p", lambda e, u=u, wd=wd, first=first, last=last:
-               e.matmul(bank[ACC][:, 0:wd], T.I128[:], T.cmp[:, u:u + wd], first, last),
-               r=[("cmp", u, u + wd), ("I128", 0, 128)], x=["b3"])
-            if first:
-                st["first"] = False
-                key_sub(t)
-        if st["done"] == W:
-            st["done"] = 0
-            st["first"] = True
+    def turn_block(src, name, b, tb, slot):
+        op("p", lambda e: e.transpose(turn[tb][:, 128 * slot:128 * slot + 128], src[:, 128 * b:128 * b + 128], T.I[:, 0:128]),
+           r=[(name, 128 * b, 128 * b + 128), ("I", 0, 128)], x=["t%d" % tb])
 
-    def compare(src, name, a, b, t):
-        op("v", lambda e: e.tensor_tensor(T.cmp[:, a:b], src[:, a:b], T.thr[:, a:b], A.is_gt),
-           r=[(name, a, b)], w=[("cmp", a, b)], x=thr_banks(a, b))
-        add_up(a, b, t)
+    def compare(b, tb, slot, m, at, sign):
+        op("v", lambda e: e.tensor_scalar(T.cm[:, at:at + 128 * m], turn[tb][:, 128 * slot:128 * (slot + m)], sign, T.th[:, b:b + 1], A.mult, A.is_gt),
+           r=[("th", b, b + 1)], w=[("cm", at, at + 128 * m)], x=["t%d" % tb])
+
+    def add_up(at):
+        into_sum(T.cm[:, at:at + 128], T.cb[:, 0:1], [("cm", at, at + 128), ("cb", 0, 1)])
 
     def key0(t):
         op("v", lambda e: e.tensor_scalar(T.rk[:], T.M16[:], T.Kb[:, t:t + 1], None, A.mult),
            r=[("M16", 0, 16), ("Kb", t, t + 1)], w=[("rk", 0, 16)])
 
     def key1():
-        op("p", lambda e: e.matmul(bank[ACC][:, 128:144], T.G[:], T.rk[:], True, True), r=[("G", 0, 128), ("rk", 0, 16)], x=["b3"])
+        op("p", lambda e: e.matmul(bank[ACC][:, 16:32], T.G[:], T.rk[:], True, True), r=[("G", 0, 128), ("rk", 0, 16)], x=XA)
 
     def key2(t):
-        op("v", lambda e: e.tensor_reduce(T.sm[:, 4:5], bank[ACC][:, 128:144], AxisListType.X, A.max), w=[("sm", 4, 5)], x=["b3"])
+        op("v", lambda e: e.tensor_reduce(T.sm[:, 4:5], bank[ACC][:, 16:32], AxisListType.X, A.max), w=[("sm", 4, 5)], x=XA)
         op("v", lambda e: e.tensor_scalar(T.Z[:], T.Zoff[:], T.Kb[:, t:t + 1], T.sm[:, 4:5], A.add, A.is_ge),
-           r=[("Zoff", 0, 144), ("Kb", t, t + 1), ("sm", 4, 5)], w=[("Z", 0, 144)])
+           r=[("Zoff", 0, 8), ("Kb", t, t + 1), ("sm", 4, 5)], w=[("Z", 0, 8)])
 
-    def elect_mm(k, bi):
-        a, b = PAR["eb"][k], PAR["eb"][k + 1]
-        wd = (b - a) // 16
+    def elect_pick(k, bi):
+        a = 2048 * k
         for i in range(16):
-            op("p", lambda e, i=i: e.matmul(bank[bi][:, 256:256 + wd], T.Z[:, 15 - i:143 - i], T.p[:, a + i:b:16], i == 0, i == 15),
-               r=[("Z", 0, 144), ("p", a, b)], x=["b%d" % bi])
+            op("p", lambda e, i=i: e.matmul(bank[bi][:, i:128:16], T.p[:, a + i:a + 2048:16], T.Z[:], True, True),
+               r=[("Z", 0, 8), ("p", a, a + 2048)], x=["b%d" % bi])
+
+    def elect_copy(k, bi, q):
+        out = T.es[:, 128 * k:128 * k + 128]
+        if q == "v":
+            op("v", lambda e: e.tensor_copy(out, bank[bi][:, 0:128]), w=[("es", k, k + 1)], x=["b%d" % bi])
+        else:
+            op("s", lambda e: e.activation(out, bank[bi][:, 0:128], F.Copy), w=[("es", k, k + 1)], x=["b%d" % bi])
+
+    def elect_turn(k, bi):
+        op("p", lambda e: e.matmul(bank[bi][:, 128:256], T.es[:, 128 * k:128 * k + 128], T.I[:, 0:128], True, True),
+           r=[("es", k, k + 1), ("I", 0, 128)], x=["b%d" % bi])
 
     def elect_ln(k, bi):
         j0, j1 = PAR["eb"][k] // 16, PAR["eb"][k + 1] // 16
-        op("s", lambda e: e.activation(T.lnx[:, j0:j1], bank[bi][:, 256:256 + j1 - j0], F.Ln), w=[("lnx", j0, j1)], x=["b%d" % bi])
+        op("s", lambda e: e.activation(T.lnx[:, j0:j1], bank[bi][:, 128:128 + j1 - j0], F.Ln), w=[("lnx", j0, j1)], x=["b%d" % bi])
 
     def elect_round(k, rnd):
         j0, j1 = PAR["eb"][k] // 16, PAR["eb"][k + 1] // 16
@@ -191,27 +296,30 @@ def rank_program(g, core, T, topo):
             src = T.cores[(rank + 1 + rnd % (n - 1)) % n]
             op(None, None, w=[("land%d" % rnd, 0, KB)], ch="arr%d" % rnd, inc=len(topo.engines(src, core)))
 
-    def decide(t, split):
-        op("v", lambda e: e.tensor_reduce(T.sm[:, 8:9], bank[ACC][:, 0:NR], AxisListType.X, A.add), w=[("sm", 8, 9)], x=["b3"])
-        op("v", lambda e: e.tensor_scalar(T.DX[:], T.X[:], T.sm[:, 8:9], 0.0, A.mult, A.is_gt),
-           r=[("X", 0, 256), ("sm", 8, 9)], w=[("DX", 0, 256)])
-        op("v", lambda e: e.tensor_scalar(T.Kb[:, t + 1:t + 2], T.sm[:, 8:9], -64.0, T.Kb[:, t:t + 1], A.max, A.add),
-           r=[("sm", 8, 9), ("Kb", t, t + 1)], w=[("Kb", t + 1, t + 2)])
-        if split:
-            op("v", lambda e: e.tensor_scalar(T.nb[:, 0:1], T.sm[:, 8:9], 0.0, -1.0, A.is_gt, A.mult), r=[("sm", 8, 9)], w=[("nb", 0, 1)])
-            op("v", lambda e: e.tensor_scalar(T.nb[:, 2:3], T.sm[:, 8:9], 0.0, -1.0, A.is_lt, A.mult), r=[("sm", 8, 9)], w=[("nb", 2, 3)])
+    def fill(step, a, b, bi):
+        j = 128 * (2 + shifts.index(shift_of(step, a)))
+        op("p", lambda e: e.matmul(bank[bi][:, 0:b - a], T.I[:, j:j + 128], T.h[:, a:b], True, False),
+           r=[("I", j, j + 128), ("h", a, b)], x=["b%d" % bi])
 
-    def pick(a, b, bi):
-        op("p", lambda e: e.matmul(bank[bi][:, 0:b - a], T.DX[:, 0:128], T.h[:, a:b], True, False),
-           r=[("DX", 0, 128), ("h", a, b)], x=["b%d" % bi])
-        op("p", lambda e: e.matmul(bank[bi][:, 0:b - a], T.DX[:, 128:256], T.p[:, a:b], False, True),
-           r=[("DX", 128, 256), ("p", a, b)], x=["b%d" % bi])
+    def kept(a, b, bi):
+        op("p", lambda e: e.matmul(bank[bi][:, 0:b - a], T.D[:], T.p[:, a:b], False, True),
+           r=[("D", 0, 128), ("p", a, b)], x=["b%d" % bi])
 
-    def phase(plan, oname, rnd, t):
-        for it in plan:
+    def phase(key, rnd, t):
+        step = t % 2
+        if key in ("g0", "g1"):
+            st["done"], st["all"] = 0, 1 + sum(len(s) for s in PAR["sets"][step])
+        for it in PAR[key]:
+            if t == 2 * RO - 1 and key == "g1" and it[0] == "pf":
+                continue
             k = it[0]
+            FOOT["tag"] = (key, t, it)
             if k == "em":
-                elect_mm(it[1], it[2])
+                elect_pick(it[1], it[2])
+            elif k in ("ev", "es"):
+                elect_copy(it[1], it[2], k[1])
+            elif k == "et":
+                elect_turn(it[1], it[2])
             elif k == "el":
                 elect_ln(it[1], it[2])
             elif k == "er":
@@ -222,102 +330,141 @@ def rank_program(g, core, T, topo):
                 key1()
             elif k == "k2":
                 key2(t + 1)
+            elif k == "d":
+                op("v", lambda e: e.tensor_scalar(T.D[:], T.X[:], acc, BIG, A.is_ge, A.mult), r=[("X", 0, 128)], w=[("D", 0, 128)], x=XA)
+            elif k == "k":
+                op("v", lambda e: e.tensor_scalar(T.Kb[:, t + 1:t + 2], acc, 0.0, T.Kb[:, t:t + 1], A.max, A.add),
+                   r=[("Kb", t, t + 1)], w=[("Kb", t + 1, t + 2)], x=XA)
+            elif k == "u":
+                op("v", lambda e: e.tensor_scalar(unit2, acc, 0.0, 1.0 / BIG, A.is_gt, A.max), w=[("nb", 0, 1)], x=XA)
+            elif k == "us":
+                op("s", lambda e: e.activation(unit, unit2, F.Copy), r=[("nb", 0, 1)], w=[("sm", 8, 9)])
+            elif k == "nb":
+                op("v", lambda e: e.tensor_scalar(nkeep, acc, 0.0, -1.0, A.is_le, A.mult), w=[("nb", 2, 3)], x=XA)
+            elif k == "y0":
+                op("v", lambda e: e.tensor_scalar(T.ec[:, 0:1], T.Kb[:, t + 1:t + 2], T.cb[:, 2:3], -1.0 / 128, A.subtract, A.mult),
+                   r=[("Kb", t + 1, t + 2), ("cb", 2, 3)], w=[("ec", 0, 1)])
+            elif k == "y1":
+                op("p", lambda e: e.matmul(bank[ACC][0:1, 0:128], T.ec[:, 0:1], T.negI[:], True, True),
+                   r=[("ec", 0, 1), ("negI", 0, 128)], x=XA)
+            elif k == "y2":
+                op("v", lambda e: e.tensor_copy(T.dif[0:1, :], bank[ACC][0:1, 0:128]), w=[("dif", 0, 128)], x=XA)
+                op("y", lambda e: e.dma_start(T.ye[:], T.dif[0:1, :]), r=[("dif", 0, 128)], ch="stored", inc=16)
+            elif k == "t":
+                for i in range(it[2], it[3]):
+                    tb, slot, _ = slot_of(step, i)
+                    turn_block(T.h, "h", PAR["sets"][step][i][it[1]], tb, slot + it[1])
+            elif k == "c":
+                for i in range(it[1], it[2]):
+                    tb, slot, at = slot_of(step, i)
+                    compare(PAR["sets"][step][i][0], tb, slot, len(PAR["sets"][step][i]), at, -1.0)
+            elif k == "n":
+                for u in range(slot_of(step, it[1])[2], slot_of(step, it[2])[2], 128):
+                    add_up(u)
+            elif k == "r":
+                op("v", lambda e, bi=it[1]: e.tensor_tensor_scan(T.run[:, 0:mw], bank[bi][:, 0:mw], T.run[:, 128:128 + mw], T.Kb[:, t:t + 1], A.add, A.add),
+                   r=[("run", 128, 256), ("Kb", t, t + 1)], w=[("run", 0, mw)], x=["b%d" % it[1]])
+            elif k == "j":
+                into_sum(T.negI[:], T.run[:, mw - 1:mw], [("run", 0, mw), ("negI", 0, 128)])
             else:
                 a, b = it[1], it[2]
                 if k in ("gv", "gs", "tg"):
-                    offs = T[oname]
-                    rd = [("p", 0, W), (oname, a // 16, b // 16)]
-                    win = T.p[:, 0:W].indirect(offs[:, a // 16:b // 16])
+                    name = ("off%d", "land%d")[step] % rnd
+                    rd = [("p", 0, W), (name, a // 16, b // 16)]
+                    win = T.p[:, 0:W].indirect(T[name][:, a // 16:b // 16])
+                    sc = -2.0 ** -shift_of(step, a)
                 if k == "gv":
-                    op("v", lambda e, a=a, b=b, win=win: e.tensor_copy(T.h[:, a:b], win), r=rd, w=[("h", a, b)])
+                    op("v", lambda e, a=a, b=b, win=win, sc=sc: e.tensor_scalar(T.h[:, a:b], win, sc, None, A.mult), r=rd, w=[("h", a, b)])
                 elif k == "gs":
-                    op("s", lambda e, a=a, b=b, win=win: e.activation(T.h[:, a:b], win, F.Copy), r=rd, w=[("h", a, b)])
+                    op("s", lambda e, a=a, b=b, win=win, sc=sc: e.activation(T.h[:, a:b], win, F.Copy, scale=sc), r=rd, w=[("h", a, b)])
                 elif k == "tg":
-                    op("v", lambda e, a=a, b=b, win=win: e.tensor_tensor(T.cmp[:, a:b], win, T.ths[:, a:b], A.is_gt),
-                       r=rd + [("ths", a, b)], w=[("cmp", a, b)])
-                    add_up(a, b, t)
-                elif k == "tv":
-                    op("v", lambda e, a=a, b=b: e.tensor_copy(T.ths[:, a:b], T.thr[:, a:b]), w=[("ths", a, b)], x=thr_banks(a, b))
-                elif k == "c":
-                    compare(T.h, "h", a, b, t)
-                elif k == "pe":
-                    bi = it[3]
-                    pick(a, b, bi)
-                    if it[4] == "s":
-                        op("s", lambda e, a=a, b=b, bi=bi: e.activation(T.p[:, a:b], bank[bi][:, 0:b - a], F.Copy),
-                           w=[("p", a, b)], x=["b%d" % bi])
-                    else:
-                        op("v", lambda e, a=a, b=b, bi=bi: e.tensor_copy(T.p[:, a:b], bank[bi][:, 0:b - a]),
-                           w=[("p", a, b)], x=["b%d" % bi])
+                    op("v", lambda e, a=a, b=b, win=win: e.tensor_tensor(T.fb[:, a:b], win, T.ths[:, a:b], A.is_gt),
+                       r=rd + [("ths", a, b)], w=[("fb", a, b)])
+                elif k == "m":
+                    for u in range(a, b, mw):
+                        first, last = u == PAR["direct"][step][0], u + mw == PAR["direct"][step][1]
+                        op("p", lambda e, u=u, first=first, last=last, bi=it[3]:
+                           e.matmul(bank[bi][:, 0:mw], T.I[:, 128:256], T.fb[:, u:u + mw], first, last),
+                           r=[("fb", u, u + mw), ("I", 128, 256)], x=["b%d" % it[3]])
+                elif k == "pf":
+                    fill(step, a, b, it[3])
+                elif k == "pk":
+                    kept(a, b, it[3])
+                elif k == "cs":
+                    op("s", lambda e, a=a, b=b, bi=it[3]: e.activation(T.p[:, a:b], bank[bi][:, 0:b - a], F.Copy, scale=unit),
+                       r=[("sm", 8, 9)], w=[("p", a, b)], x=["b%d" % it[3]])
+                elif k == "cv":
+                    op("v", lambda e, a=a, b=b, bi=it[3]: e.tensor_scalar(T.p[:, a:b], bank[bi][:, 0:b - a], unit, None, A.mult),
+                       r=[("sm", 8, 9)], w=[("p", a, b)], x=["b%d" % it[3]])
                 elif k == "va":
-                    op("v", lambda e, a=a, b=b: e.tensor_scalar(T.h[:, a:b], T.h[:, a:b], T.nb[:, 0:1], T.nb[:, 2:3], A.mult, A.add),
+                    op("v", lambda e, a=a, b=b: e.tensor_scalar(T.h[:, a:b], T.h[:, a:b], unit2, nkeep, A.mult, A.add),
                        r=[("h", a, b), ("nb", 0, 3)], w=[("h", a, b)])
                 elif k == "vb":
-                    op("v", lambda e, a=a, b=b: e.tensor_scalar(T.cmp[:, a:b], T.p[:, a:b], T.nb[:, 2:3], T.nb[:, 0:1], A.mult, A.add),
-                       r=[("p", a, b), ("nb", 0, 3)], w=[("cmp", a, b)])
+                    op("v", lambda e, a=a, b=b: e.tensor_scalar(T.fb[:, a:b], T.p[:, a:b], nkeep, unit2, A.mult, A.subtract),
+                       r=[("p", a, b), ("nb", 0, 3)], w=[("fb", a, b)])
+                elif k == "vc":
+                    op("v", lambda e, a=a, b=b: e.tensor_tensor_scan(T.p[:, a:b], T.h[:, a:b], T.fb[:, a:b], 1.0, A.min, A.mult),
+                       r=[("fb", a, b), ("h", a, b)], w=[("p", a, b)])
+                elif k == "ln":
+                    op("s", lambda e, a=a, b=b, bi=it[3]: e.activation(T.lin[:, a:b], bank[bi][:, 0:b - a], F.Ln, scale=unit),
+                       r=[("sm", 8, 9)], w=[("lin", a, b)], x=["b%d" % it[3]])
+                elif k == "rs":
+                    op("s", lambda e, a=a, b=b: e.activation(T.lin[:, a:b], T.lin[:, a:b], F.Identity, bias=MAGIC + MID, scale=1.0 / C),
+                       r=[("lin", a, b)], w=[("lin", a, b)])
+                elif k == "rv":
+                    op("v", lambda e, a=a, b=b: e.tensor_scalar(T.lin[:, a:b], T.lin[:, a:b], 1.0 / C, MAGIC + MID, A.mult, A.add),
+                       r=[("lin", a, b)], w=[("lin", a, b)])
+                elif k == "sv":
+                    op("v", lambda e, a=a, b=b: e.tensor_scalar(T.lin[:, a:b], T.lin[:, a:b], -MAGIC, None, A.add),
+                       r=[("lin", a, b)], w=[("lin", a, b)])
                 else:
-                    op("v", lambda e, a=a, b=b: e.tensor_tensor_scan(T.p[:, a:b], T.h[:, a:b], T.cmp[:, a:b], 1.0, A.min, A.mult),
-                       r=[("cmp", a, b), ("h", a, b)], w=[("p", a, b)])
+                    op("y", lambda e, a=a, b=b: e.dma_start(T.yg[:, a:b], T.lin[:, a:b]), r=[("lin", a, b)], ch="stored", inc=16)
+
+    if "only" in FOOT:
+        key, t, it = FOOT["only"]
+        del ops[:]
+        keep = PAR[key]
+        PAR[key] = [it]
+        phase(key, (t + 1) // 2 if key[0] in "es" else t // 2, t)
+        PAR[key] = keep
+        return FOOT["hook"](ops)
 
     sub = PAR["sub"]
+    into_sum(T.I[:, 0:128], T.cb[:, 2:3], [("I", 0, 128), ("cb", 2, 3)])
+    pend = []
     for k in range(len(sub) - 1):
         a, b = sub[k], sub[k + 1]
-        op("s", lambda e, a=a, b=b: e.activation(T.p[:, a:b], T.raw[:, a:b], F.Exp, bias=-C * MID, scale=C),
+        op("s", lambda e, a=a, b=b: e.activation(T.p[:, a:b], T.raw[:, a:b], F.Exp, bias=ENC, scale=C),
            r=[("raw", a, b)], w=[("p", a, b)])
-        compare(T.p, "p", a, b, -1)
+        blocks = range(a // 128, (b + 127) // 128)
+        for u in blocks:
+            turn_block(T.p, "p", u, k % 2, u - a // 128)
+        for u in pend:
+            add_up(128 * u)
+        for u in blocks:
+            compare(u, k % 2, u - a // 128, 1, 128 * u, 1.0)
+        pend = blocks
+    for u in pend:
+        add_up(128 * u)
     op("s", lambda e: e.activation(T.sm[:, 2:3], T.sm[:, 1:2], F.Ln), r=[("sm", 1, 2)], w=[("sm", 2, 3)])
-    op("v", lambda e: e.tensor_reduce(T.Kb[:, 0:1], bank[ACC][:, 0:NR], AxisListType.X, A.add), w=[("Kb", 0, 1)], x=["b3"])
-    key0(0)
+    op("v", lambda e: e.tensor_scalar(T.rk[:], T.M16[:], acc, None, A.mult), r=[("M16", 0, 16)], w=[("rk", 0, 16)], x=XA)
+    op("v", lambda e: e.tensor_copy(T.Kb[:, 0:1], acc), w=[("Kb", 0, 1)], x=XA)
     key1()
     key2(0)
-    phase(PAR["e0"], None, 0, -1)
+    phase("e0", 0, -1)
 
     for rnd in range(RO):
         t = 2 * rnd
-        phase(PAR["g0"], "off%d" % rnd, rnd, t)
-        decide(t, True)
-        phase(PAR["s0"], None, rnd, t)
-        phase(PAR["g1"], "land%d" % rnd, rnd, t + 1)
-        decide(t + 1, rnd < RO - 1)
+        phase("g0", rnd, t)
+        phase("s0", rnd, t)
+        phase("g1", rnd, t + 1)
         if rnd < RO - 1:
-            phase(PAR["s1"], None, rnd + 1, t + 1)
+            phase("s1", rnd + 1, t + 1)
 
-    fin = PAR["fin"]
-    lo = [0]
-
-    def finish(a, b, eng):
-        if eng == "s":
-            op("s", lambda e: e.activation(T.lin[:, a:b], T.lin[:, a:b], F.Identity, bias=MAGIC + MID, scale=1.0 / C),
-               r=[("lin", a, b)], w=[("lin", a, b)])
-        else:
-            op("v", lambda e: e.tensor_scalar(T.lin[:, a:b], T.lin[:, a:b], 1.0 / C, MAGIC + MID, A.mult, A.add),
-               r=[("lin", a, b)], w=[("lin", a, b)])
-        op("v", lambda e: e.tensor_scalar(T.lin[:, a:b], T.lin[:, a:b], -MAGIC, None, A.add), r=[("lin", a, b)], w=[("lin", a, b)])
-        if b in PAR["store"]:
-            a3 = lo[0]
-            lo[0] = b
-            op("y", lambda e: e.dma_start(T.yg[:, a3:b], T.lin[:, a3:b]), r=[("lin", a3, b)], ch="stored", inc=16)
-
-    held = []
-    for k in range(len(fin)):
-        a, b, eng = fin[k]
-        bi = k % 4
-        pick(a, b, bi)
-        op("s", lambda e, a=a, b=b, bi=bi: e.activation(T.lin[:, a:b], bank[bi][:, 0:b - a], F.Ln), w=[("lin", a, b)], x=["b%d" % bi])
-        if held:
-            finish(*held.pop())
-        if eng == "s" and k < len(fin) - 1:
-            held.append(fin[k])
-        else:
-            finish(a, b, eng)
-        if k == 0:
-            op("v", lambda e: e.tensor_scalar(T.ec[:, 0:1], T.Kb[:, 2 * RO:2 * RO + 1], T.Kb[:, 19:20], -1.0 / 128, A.add, A.mult),
-               r=[("Kb", 2 * RO, 2 * RO + 1), ("Kb", 19, 20)], w=[("ec", 0, 1)])
-        if k == PAR["yek"]:
-            op("p", lambda e: e.matmul(bank[ACC][0:1, 0:128], T.ec[:, 0:1], T.negI[:], True, True),
-               r=[("ec", 0, 1), ("negI", 0, 128)], x=["b3"])
-            op("v", lambda e: e.tensor_copy(T.dif[0:1, :], bank[ACC][0:1, 0:128]), w=[("dif", 0, 128)], x=["b3"])
-            op("y", lambda e: e.dma_start(T.ye[:], T.dif[0:1, :]), r=[("dif", 0, 128)], ch="stored", inc=16)
+    phase("fin", None, 2 * RO - 1)
+    FOOT["tag"] = None
+    if "hook" in FOOT:
+        return FOOT["hook"](ops)
 
     def meet(u, v):
         for (n1, a1, b1) in u:

import math
from concourse.mybir import AluOpType, AxisListType, ActivationFunctionType

W = 4032
WP = 4096
RO = 4
KB = W // 16
C = math.log(2.0) / 64
MID = 2016.0
ENC = C * (0.0225 - MID)
MAGIC = 12582912.0
BIG = 2.0 ** 76

PAR = {
    "sets": [[(8 + i, 12 + i) for i in range(4)] + [(16 + i, 24 + i) for i in range(8)],
             [(12 + i, i) for i in range(12)]],
    "stages": [[0, 4, 8, 10, 12], [0, 4, 8, 10, 12]],
    "direct": [(0, 1024), (3072, 4032)],
    "load": [0, 1920, 3072, 3840, 4032],
    "sub": [0, 640, 1280, 1920, 2560, 3072, 3456, 3840, 4032],
    "eb": [0, 1024, 2048, 4032],
    "e0": [("em", 0, 4), ("em", 1, 3), ("el", 0, 4), ("er", 0), ("el", 1, 3), ("er", 1)],
    "g0": [("em", 2, 4), ("tg", 0, 1024), ("gs", 1024, 1536), ("z",), ("gs", 1536, 2048), ("t", 0, 0, 4), ("el", 2, 4), ("er", 2),
           ("t", 1, 0, 4), ("m", 0, 1024, 3), ("gs", 2048, 2560), ("c", 0, 4), ("r", 3), ("gv", 2816, 3072), ("gs", 3072, 3584), ("t", 0, 4, 8), ("n", 0, 4),
           ("j",), ("t", 1, 4, 8), ("gs", 2560, 2816), ("c", 4, 8), ("gs", 3584, 3840), ("t", 0, 8, 10), ("t", 1, 8, 10), ("gs", 3840, 4032),
           ("n", 4, 8), ("c", 8, 10), ("t", 0, 10, 12), ("t", 1, 10, 12), ("gs", 0, 1024), ("n", 8, 10), ("c", 10, 12), ("pf", 1536, 2048, 0),
           ("n", 10, 12)],
    "s0": [("d",), ("nb",), ("u",), ("pk", 1536, 2048, 0), ("cs", 1536, 2048, 0), ("pf", 2048, 2560, 1), ("pk", 2048, 2560, 1),
           ("vb", 0, 1536), ("cs", 2048, 2560, 1), ("pf", 2560, 3072, 2), ("pk", 2560, 3072, 2), ("va", 0, 1536), ("cs", 2560, 3072, 2),
           ("pf", 3072, 3584, 3), ("pk", 3072, 3584, 3), ("cs", 3072, 3584, 3), ("pf", 3584, 4032, 4), ("pk", 3584, 4032, 4),
           ("vc", 0, 1536), ("cs", 3584, 4032, 4), ("k",)],
    "g1": [("tg", 3072, 4032), ("gs", 0, 512), ("z",), ("gs", 1536, 2048), ("t", 1, 0, 4), ("m", 3072, 4032, 3), ("gv", 1280, 1536),
           ("t", 0, 0, 4), ("gs", 512, 1024), ("c", 0, 4), ("r", 3), ("pf", 0, 512, 0), ("gs", 2048, 2560), ("t", 1, 4, 8), ("n", 0, 4), ("j",),
           ("t", 0, 4, 8), ("gs", 1024, 1280), ("c", 4, 8), ("gs", 2560, 2816), ("t", 1, 8, 10), ("pf", 512, 1024, 1), ("t", 0, 8, 10), ("gs", 2816, 3072),
           ("n", 4, 8), ("c", 8, 10), ("t", 1, 10, 12), ("t", 0, 10, 12), ("gs", 3072, 4032), ("n", 8, 10), ("c", 10, 12), ("pf", 1024, 1536, 2),
           ("n", 10, 12)],
    "s1": [("d",), ("u",), ("k",), ("pk", 0, 512, 0), ("k0",), ("pk", 512, 1024, 1), ("nb",), ("cs", 0, 512, 0), ("k1",),
           ("vb", 2560, 4032), ("pk", 1024, 1536, 2), ("cs", 512, 1024, 1), ("pf", 1536, 2048, 3), ("pk", 1536, 2048, 3), ("k2",),
           ("cs", 1024, 1536, 2), ("pf", 2048, 2560, 4), ("pk", 2048, 2560, 4), ("cs", 1536, 2048, 3), ("va", 2560, 4032), ("em", 0, 0),
           ("cs", 2048, 2560, 4), ("el", 0, 0), ("em", 1, 1), ("vc", 2560, 4032), ("el", 1, 1), ("er", 0), ("er", 1)],
    "fin": [(0, 256, "v"), (256, 512, "v"), (512, 1024, "v"), (1024, 1536, "s"), (1536, 2048, "v"), (2048, 2560, "s"),
            (2560, 3072, "s"), (3072, 3584, "s"), (3584, 4032, "s")],
    "store": [256, 512, 1024, 2048, 3072, 4032],
    "yek": 7,
}
PAR.update({
    "g0": [("em", 2, 4), ("gs", 1024, 1536), ("tg", 0, 1024), ("t", 0, 0, 4), ("z",), ("el", 2, 4), ("er", 2), ("gv", 3072, 3584),
           ("m", 0, 1024, 3), ("gs", 1536, 2048), ("r", 3), ("t", 1, 0, 4), ("gs", 2048, 2560), ("t", 0, 4, 8), ("t", 1, 4, 8), ("c", 0, 4),
           ("n", 0, 4), ("gs", 2560, 2816), ("t", 0, 8, 10), ("gs", 3584, 3840), ("t", 1, 8, 10), ("j",), ("c", 4, 8), ("n", 4, 8),
           ("gs", 2816, 3072), ("t", 0, 10, 12), ("gs", 3840, 4032), ("t", 1, 10, 12), ("pf", 1536, 2048, 0), ("c", 8, 10), ("n", 8, 10),
           ("gs", 0, 1024), ("c", 10, 12), ("n", 10, 12)],
    "s0": [("d",), ("pk", 1536, 2048, 0), ("pf", 2048, 2560, 1), ("u",), ("us",), ("nb",), ("vb", 0, 1536), ("pk", 2048, 2560, 1),
           ("cs", 1536, 2048, 0), ("pf", 2560, 3072, 2), ("cs", 2048, 2560, 1), ("va", 0, 1536), ("pk", 2560, 3072, 2), ("k",),
           ("pf", 3072, 3584, 3), ("pk", 3072, 3584, 3), ("pf", 3840, 4032, 0), ("vc", 0, 1536), ("cs", 2560, 3072, 2),
           ("pk", 3840, 4032, 0), ("cs", 3072, 3584, 3), ("pf", 3584, 3840, 4), ("pk", 3584, 3840, 4), ("cv", 3840, 4032, 0),
           ("cs", 3584, 3840, 4)],
    "g1": [("gv", 0, 512), ("z",), ("t", 1, 0, 4), ("pf", 0, 512, 0), ("gs", 1536, 2048), ("t", 0, 0, 4), ("gs", 512, 1024),
           ("tg", 3072, 4032), ("t", 1, 4, 8), ("gs", 2048, 2560), ("m", 3072, 4032, 3), ("gs", 1024, 1536), ("c", 0, 4), ("r", 3),
           ("t", 0, 4, 8), ("t", 1, 8, 10), ("n", 0, 4), ("c", 4, 8), ("gs", 2560, 2816), ("gs", 3072, 4032), ("t", 0, 8, 10),
           ("t", 1, 10, 12), ("j",), ("gv", 2816, 3072), ("n", 4, 8), ("t", 0, 10, 12), ("pf", 512, 1024, 1), ("c", 8, 10), ("c", 10, 12),
           ("n", 8, 10), ("n", 10, 12), ("pf", 1024, 1536, 2)],
    "s1": [("d",), ("u",), ("us",), ("pk", 0, 512, 0), ("cs", 0, 512, 0), ("pf", 1536, 2048, 3), ("nb",), ("pk", 512, 1024, 1), ("k",), ("k0",),
           ("k1",), ("pk", 1024, 1536, 2), ("vb", 2560, 4032), ("k2",), ("cs", 512, 1024, 1), ("cs", 1024, 1536, 2),
           ("pf", 2048, 2560, 4), ("pk", 1536, 2048, 3), ("pk", 2048, 2560, 4), ("cs", 1536, 2048, 3), ("va", 2560, 4032), ("em", 0, 0),
           ("em", 1, 1), ("vc", 2560, 4032), ("cs", 2048, 2560, 4), ("el", 0, 0), ("el", 1, 1), ("er", 0), ("er", 1)],
})


def last_plan(cuts, scalar_rounds, stores):
    plan = [("pf", cuts[0], cuts[1], 0), ("d",), ("u",), ("us",), ("k",), ("y0",)]
    held, lo = [], 0
    for k in range(len(cuts) - 1):
        a, b = cuts[k], cuts[k + 1]
        plan += [("pf", a, b, k % 5)] * (k > 0) + [("pk", a, b, k % 5), ("ln", a, b, k % 5)]
        ready, held = held, []
        if k in scalar_rounds and b < W:
            held = [k]
        else:
            ready = ready + [k]
        for j in ready:
            plan += [("rs" if j in scalar_rounds else "rv", cuts[j], cuts[j + 1]), ("sv", cuts[j], cuts[j + 1])]
            if cuts[j + 1] in stores:
                plan.append(("st", lo, cuts[j + 1]))
                lo = cuts[j + 1]
        plan += [("y1",), ("y2",)] * (k == 3)
    return plan


PAR.update({
    "sets": [[(i, 8 + i) for i in range(8)] + [(20 + i, 16 + i) for i in range(4)],
             [(16 + i, i) for i in range(8)] + [(24 + i, 28 + i) for i in range(4)]],
    "direct": [(3072, 4032), (1024, 2048)],
    "eb": [0, 2048, 4032], "mw": 64,
    "e0": [("em", 0, 4), ("ev", 0, 4), ("et", 0, 4), ("el", 0, 4), ("er", 0)],
'g0': [('em',1,0),('gv',0,320),('ev',1,0),('et',1,0),('gv',320,768),('gs',1024,1664),('el',1,0),('gs',1664,2048),('er',1),('t',0,0,2),('gs',768,1024),('t',1,0,2),('gs',2048,2560),('t',0,2,3),('t',0,3,6),('t',1,2,6),('c',0,2),('t',1,6,8),('gs',2560,2816),('tg',3072,3584),('n',0,1),('gs',2816,3072),('t',0,6,8),('c',2,8),('m',3072,3520,2),('tg',3584,3968),('n',1,6),('t',1,10,12),('t',1,8,10),('t',0,8,10),('m',3520,3584,2),('t',0,10,12),('m',3584,3968,2),('tg',3968,4032),('m',3968,4032,2),('c',8,11),('r',2),('gs',3072,4032),('c',11,12),('n',6,10),('j',),('n',10,12)],
's0': [('d',),('pf',0,512,0),('u',),('pk',0,512,0),('pf',512,1024,1),('us',),('pk',512,1024,1),('pf',1024,1536,2),('pk',1024,1536,2),('nb',),('k',),('pf',1536,2048,4),('vb',2560,4032),('cs',0,512,0),('cs',512,1024,1),('pk',1536,2048,4),('va',2560,2880),('cs',1024,1536,2),('pf',2176,2560,3),('va',2880,4032),('pk',2176,2560,3),('cs',1536,2048,4),('pf',2048,2176,2),('vc',2560,2880),('pk',2048,2176,2),('vc',2880,4032),('cv',2176,2560,3),('cs',2048,2176,2)],
'g1': [('gs',2048,2592),('t',0,0,4),('gv',0,672),('t',1,0,4),('gs',672,1024),('tg',1024,1536),('gs',2592,3136),('t',1,4,8),('m',1024,1536,1),('t',0,4,8),('tg',1536,2048),('m',1536,2048,1),('gs',3136,3584),('gs',3584,3840),('c',0,8),('n',0,3),('t',0,8,10),('n',3,6),('t',1,8,10),('r',1),('t',0,10,12),('gs',3840,4032),('gs',1024,1952),('t',1,10,12),('j',),('c',8,12),('n',6,12),('pf',512,1024,2),('gv',1952,2048),('pf',2816,3072,4)],
's1': [('nb',),('pf',0,512,3),('u',),('us',),('d',),('pk',0,512,3),('k',),('vb',1024,2048),('pk',512,1024,2),('k0',),('k1',),('pf',3584,4032,1),('va',1024,2048),('pk',3584,4032,1),('cs',0,512,3),('pf',3072,3584,0),('pk',3072,3584,0),('k2',),('vc',1024,2048),('vb',2048,2816),('cs',512,1024,2),('em',0,2),('va',2048,2816),('pk',2816,3072,4),('cs',3584,4032,1),('ev',0,2),('cs',3072,3584,0),('vc',2048,2816),('et',0,2),('cs',2816,3072,4),('el',0,2),('er',0)],
'stages': [[0,2,6,10,12],[0,4,8,10,12]],
    "fin": last_plan([0, 160, 512, 1024, 1504, 1696, 2048, 2560, 3072, 3584, 3840, 4032], (3, 4, 7, 8, 9, 10), (160, 512, 1024, 2048, 3072, 4032)),
})
FOOT = {}

SCRATCH = {
    "raw": ("sbuf", [128, W], "int32"),
    "lin": ("sbuf", [128, W], "float32"),
    "p": ("sbuf", [128, WP], "bfloat16"),
    "h": ("sbuf", [128, WP], "bfloat16"),
    "cm": ("sbuf", [128, WP], "bfloat16"),
    "fb": ("sbuf", [128, WP], "bfloat16"),
    "ths": ("sbuf", [128, W], "bfloat16"),
    "th": ("sbuf", [128, 32], "bfloat16"),
    "nb": ("sbuf", [128, 4], "bfloat16"),
    "dif": ("sbuf", [128, 128], "float32"),
    "ci": ("sbuf", [128, 144], "int32"),
    "cj": ("sbuf", [128, 144], "int32"),
    "I": ("sbuf", [128, 1024], "bfloat16"),
    "X": ("sbuf", [128, 128], "bfloat16"),
    "D": ("sbuf", [128, 128], "bfloat16"),
    "negI": ("sbuf", [128, 128], "float32"),
    "G": ("sbuf", [128, 128], "float32"),
    "M16": ("sbuf", [128, 16], "float32"),
    "rk": ("sbuf", [128, 16], "float32"),
    "Zoff": ("sbuf", [128, 8], "bfloat16"),
    "Z": ("sbuf", [128, 8], "bfloat16"),
    "es": ("sbuf", [128, 256], "bfloat16"),
    "run": ("sbuf", [128, 256], "float32"),
    "Kb": ("sbuf", [128, 16], "float32"),
    "cb": ("sbuf", [128, 4], "bfloat16"),
    "sm": ("sbuf", [128, 16], "float32"),
    "ec": ("sbuf", [128, 4], "float32"),
    "lnx": ("sbuf", [128, 256], "float32"),
    "t0": ("psum", [128, 1024], "bfloat16"),
    "t1": ("psum", [128, 1024], "bfloat16"),
}
for _b in range(6):
    SCRATCH["b%d" % _b] = ("psum", [128, 512], "float32")
for _t in range(RO):
    SCRATCH["off%d" % _t] = ("sbuf", [128, 256], "uint16")
    SCRATCH["land%d" % _t] = ("sbuf", [128, 256], "uint16")

SEMAPHORES = (["cv", "cs", "cp", "cg", "sent", "stored"] + ["arr%d" % t for t in range(RO)]
              + ["ld%d" % k for k in range(8)])

A = AluOpType
F = ActivationFunctionType


def shift_of(step, a):
    for s in PAR["sets"][step]:
        if a // 128 in s:
            return 2 * (a // 128 - s[0])
    return 0


def slot_of(step, i):
    sets, stages = PAR["sets"][step], PAR["stages"][step]
    k = max(k for k in range(len(stages)) if stages[k] <= i)
    return k % 2, sum(len(s) for s in sets[stages[k]:i]), 128 * sum(len(s) for s in sets[:i])


def rank_program(g, core, T, topo):
    rank = T.rank_of(core)
    if rank is None:
        return
    n = len(T.cores)
    Q = {"v": g.vector, "s": g.scalar, "p": g.tensor, "g": g, "y": g.sync}
    ops = []

    def op(q, fn, r=(), w=(), x=(), ch=None, inc=1):
        ops.append({"q": q, "fn": fn, "r": list(r), "w": list(w), "x": list(x), "ch": ch, "inc": inc, "tag": FOOT.get("tag")})

    bank = [T["b%d" % k] for k in range(6)]
    turn = [T.t0, T.t1]
    ACC = 5
    acc = bank[ACC][:, 0:1]
    XA = ["b%d" % ACC]
    unit = T.sm[:, 8:9]
    unit2 = T.nb[:, 0:1]
    nkeep = T.nb[:, 2:3]
    shifts = sorted(set(shift_of(s, a) for s in (0, 1) for a in range(0, W, 128)))
    mw = PAR["mw"]
    mults = [1.0, -128.0] + [-2.0 ** sh for sh in shifts]

    ld = PAR["load"]
    for k in range(len(ld) - 1):
        a, b = ld[k], ld[k + 1]
        op("y", lambda e, a=a, b=b: e.dma_start(T.raw[:, a:b], T.g0[:, a:b]), w=[("raw", a, b)], ch="ld%d" % k, inc=16)

    def count_up(out, name, a, b, pattern, base, by):
        op("g", lambda e: e.iota(out, pattern, base, by, allow_small_or_imprecise_dtypes=True), w=[(name, a, b)])

    count_up(T.lnx[:, 0:32], "lnx", 0, 32, [[128, 32]], 0, 1)
    count_up(T.dif[:], "dif", 0, 128, [[-1, 128]], 0, 1)
    count_up(T.cb[:, 2:3], "cb", 2, 3, [[0, 1]], 127, -1)
    op("g", lambda e: e.iota(T.ci[:, 0:128], [[-16, 8], [0, 16]], 0, 1), w=[("ci", 0, 128)])
    op("g", lambda e: e.iota(T.ci[:, 128:144], [[-1, 16]], 16, 1), w=[("ci", 128, 144)])
    op("v", lambda e: e.memset(T.sm[:, 0:1], 0.0), w=[("sm", 0, 1)])
    op("s", lambda e: e.activation(T.th[:], T.lnx[:, 0:32], F.Exp, bias=ENC, scale=C), r=[("lnx", 0, 32)], w=[("th", 0, 32)])
    op("s", lambda e: e.activation(T.sm[:, 1:2], T.sm[:, 0:1], F.Exp, bias=-C * MID, scale=C),
       r=[("sm", 0, 1)], w=[("sm", 1, 2)])
    (a0, b0), (a1, b1) = sorted(PAR["direct"])
    count_up(T.lnx[:, 64:128], "lnx", 64, 128, [[1, 64]], a0, 0)
    op("s", lambda e: e.activation(T.ths[:, a0:a0 + 64], T.lnx[:, 64:128], F.Exp, bias=ENC, scale=C), r=[("lnx", 64, 128)], w=[("ths", a0, a0 + 64)])

    def octaves(a, b, back):
        op("v", lambda e: e.tensor_scalar(T.ths[:, a:b], T.ths[:, a - back:b - back], 2.0 ** (back // 64), None, A.mult),
           r=[("ths", a - back, b - back)], w=[("ths", a, b)])

    def more_codes():
        wd = 64
        while a0 + wd < b0:
            octaves(a0 + wd, min(b0, a0 + 2 * wd), wd)
            wd *= 2
        octaves(a1, b1, a1 - a0)

    op("v", lambda e: e.memset(T.p[:, W:WP], 0.0), w=[("p", W, WP)])
    op("v", lambda e: e.memset(T.h[:, W:WP], 0.0), w=[("h", W, WP)])
    op("v", lambda e: e.memset(T.cb[:, 0:1], 128.0), w=[("cb", 0, 1)])
    for j, val in enumerate(mults):
        op("v", lambda e, j=j, val=val: e.tensor_scalar(T.I[:, 128 * j:128 * j + 128], T.dif[:], 0.0, val, A.is_equal, A.mult),
           r=[("dif", 0, 128)], w=[("I", 128 * j, 128 * j + 128)])
    op("v", lambda e: e.tensor_scalar(T.X[:], T.dif[:], 0.0, -1.0e9, A.not_equal, A.mult), r=[("dif", 0, 128)], w=[("X", 0, 128)])
    op("v", lambda e: e.tensor_scalar(T.negI[:], T.dif[:], 0.0, -1.0, A.is_equal, A.mult), r=[("dif", 0, 128)], w=[("negI", 0, 128)])
    op("v", lambda e: e.tensor_scalar(T.cj[:, 0:128], T.ci[:, 0:128], 4, None, A.arith_shift_right), r=[("ci", 0, 128)], w=[("cj", 0, 128)])
    op("v", lambda e: e.tensor_scalar(T.cj[:, 128:144], T.ci[:, 128:144], 15, None, A.bitwise_and), r=[("ci", 128, 144)], w=[("cj", 128, 144)])
    op("v", lambda e: e.tensor_scalar(T.G[:], T.cj[:, 0:128], 0.0, None, A.is_equal), r=[("cj", 0, 128)], w=[("G", 0, 128)])
    op("v", lambda e: e.tensor_scalar(T.Zoff[:], T.cj[:, 0:128:16], 0.0, -1.0e9, A.not_equal, A.mult), r=[("cj", 0, 128)], w=[("Zoff", 0, 8)])
    op("v", lambda e: e.tensor_scalar(T.M16[:], T.cj[:, 128:144], 0.0, None, A.is_equal), r=[("cj", 128, 144)], w=[("M16", 0, 16)])
    op("v", lambda e: e.memset(T.run[:, 129:256], 0.0), w=[("run", 129, 256)])
    op("v", lambda e: e.tensor_scalar(T.run[:, 128:129], T.cb[:, 2:3], -1.0, None, A.mult), r=[("cb", 2, 3)], w=[("run", 128, 129)])
    more_codes()

    st = {"done": 0, "all": 33}

    def into_sum(lhs, rhs, reads):
        st["done"] += 1
        first, last = st["done"] == 1, st["done"] == st["all"]
        op("p", lambda e: e.matmul(acc, lhs, rhs, first, last), r=reads, x=XA)

    def turn_block(src, name, b, tb, slot):
        op("p", lambda e: e.transpose(turn[tb][:, 128 * slot:128 * slot + 128], src[:, 128 * b:128 * b + 128], T.I[:, 0:128]),
           r=[(name, 128 * b, 128 * b + 128), ("I", 0, 128)], x=["t%d" % tb])

    def compare(b, tb, slot, m, at, sign):
        op("v", lambda e: e.tensor_scalar(T.cm[:, at:at + 128 * m], turn[tb][:, 128 * slot:128 * (slot + m)], sign, T.th[:, b:b + 1], A.mult, A.is_gt),
           r=[("th", b, b + 1)], w=[("cm", at, at + 128 * m)], x=["t%d" % tb])

    def add_up(at):
        into_sum(T.cm[:, at:at + 128], T.cb[:, 0:1], [("cm", at, at + 128), ("cb", 0, 1)])

    def key0(t):
        op("v", lambda e: e.tensor_scalar(T.rk[:], T.M16[:], T.Kb[:, t:t + 1], None, A.mult),
           r=[("M16", 0, 16), ("Kb", t, t + 1)], w=[("rk", 0, 16)])

    def key1():
        op("p", lambda e: e.matmul(bank[ACC][:, 16:32], T.G[:], T.rk[:], True, True), r=[("G", 0, 128), ("rk", 0, 16)], x=XA)

    def key2(t):
        op("v", lambda e: e.tensor_reduce(T.sm[:, 4:5], bank[ACC][:, 16:32], AxisListType.X, A.max), w=[("sm", 4, 5)], x=XA)
        op("v", lambda e: e.tensor_scalar(T.Z[:], T.Zoff[:], T.Kb[:, t:t + 1], T.sm[:, 4:5], A.add, A.is_ge),
           r=[("Zoff", 0, 8), ("Kb", t, t + 1), ("sm", 4, 5)], w=[("Z", 0, 8)])

    def elect_pick(k, bi):
        a = 2048 * k
        for i in range(16):
            op("p", lambda e, i=i: e.matmul(bank[bi][:, i:128:16], T.p[:, a + i:a + 2048:16], T.Z[:], True, True),
               r=[("Z", 0, 8), ("p", a, a + 2048)], x=["b%d" % bi])

    def elect_copy(k, bi, q):
        out = T.es[:, 128 * k:128 * k + 128]
        if q == "v":
            op("v", lambda e: e.tensor_copy(out, bank[bi][:, 0:128]), w=[("es", k, k + 1)], x=["b%d" % bi])
        else:
            op("s", lambda e: e.activation(out, bank[bi][:, 0:128], F.Copy), w=[("es", k, k + 1)], x=["b%d" % bi])

    def elect_turn(k, bi):
        op("p", lambda e: e.matmul(bank[bi][:, 128:256], T.es[:, 128 * k:128 * k + 128], T.I[:, 0:128], True, True),
           r=[("es", k, k + 1), ("I", 0, 128)], x=["b%d" % bi])

    def elect_ln(k, bi):
        j0, j1 = PAR["eb"][k] // 16, PAR["eb"][k + 1] // 16
        op("s", lambda e: e.activation(T.lnx[:, j0:j1], bank[bi][:, 128:128 + j1 - j0], F.Ln), w=[("lnx", j0, j1)], x=["b%d" % bi])

    def elect_round(k, rnd):
        j0, j1 = PAR["eb"][k] // 16, PAR["eb"][k + 1] // 16
        off = T["off%d" % rnd]
        op("v", lambda e: e.tensor_scalar(off[:, j0:j1], T.lnx[:, j0:j1], T.sm[:, 2:3], 1.0 / C, A.subtract, A.mult),
           r=[("lnx", j0, j1), ("sm", 2, 3)], w=[("off%d" % rnd, j0, j1)])
        if j1 == KB:
            dst = T.cores[(rank - 1 - rnd % (n - 1)) % n]
            rid, pid, _ = topo.addr(dst)
            op("g", lambda e: e.remote_dma(T["land%d" % rnd][:, 0:KB], off[:, 0:KB], T.sem["arr%d" % rnd], T.sem.sent,
                                           pid, rid, topo.mask(core, dst)),
               r=[("off%d" % rnd, 0, KB)], ch="sent", inc=len(topo.engines(core, dst)))
            src = T.cores[(rank + 1 + rnd % (n - 1)) % n]
            op(None, None, w=[("land%d" % rnd, 0, KB)], ch="arr%d" % rnd, inc=len(topo.engines(src, core)))

    def fill(step, a, b, bi):
        j = 128 * (2 + shifts.index(shift_of(step, a)))
        op("p", lambda e: e.matmul(bank[bi][:, 0:b - a], T.I[:, j:j + 128], T.h[:, a:b], True, False),
           r=[("I", j, j + 128), ("h", a, b)], x=["b%d" % bi])

    def kept(a, b, bi):
        op("p", lambda e: e.matmul(bank[bi][:, 0:b - a], T.D[:], T.p[:, a:b], False, True),
           r=[("D", 0, 128), ("p", a, b)], x=["b%d" % bi])

    def phase(key, rnd, t):
        step = t % 2
        if key in ("g0", "g1"):
            st["done"], st["all"] = 0, 1 + sum(len(s) for s in PAR["sets"][step])
        for it in PAR[key]:
            if t == 2 * RO - 1 and key == "g1" and it[0] == "pf":
                continue
            k = it[0]
            FOOT["tag"] = (key, t, it)
            if k == "em":
                elect_pick(it[1], it[2])
            elif k in ("ev", "es"):
                elect_copy(it[1], it[2], k[1])
            elif k == "et":
                elect_turn(it[1], it[2])
            elif k == "el":
                elect_ln(it[1], it[2])
            elif k == "er":
                elect_round(it[1], rnd)
            elif k == "k0":
                key0(t + 1)
            elif k == "k1":
                key1()
            elif k == "k2":
                key2(t + 1)
            elif k == "d":
                op("v", lambda e: e.tensor_scalar(T.D[:], T.X[:], acc, BIG, A.is_ge, A.mult), r=[("X", 0, 128)], w=[("D", 0, 128)], x=XA)
            elif k == "k":
                op("v", lambda e: e.tensor_scalar(T.Kb[:, t + 1:t + 2], acc, 0.0, T.Kb[:, t:t + 1], A.max, A.add),
                   r=[("Kb", t, t + 1)], w=[("Kb", t + 1, t + 2)], x=XA)
            elif k == "u":
                op("v", lambda e: e.tensor_scalar(unit2, acc, 0.0, 1.0 / BIG, A.is_gt, A.max), w=[("nb", 0, 1)], x=XA)
            elif k == "us":
                op("s", lambda e: e.activation(unit, unit2, F.Copy), r=[("nb", 0, 1)], w=[("sm", 8, 9)])
            elif k == "nb":
                op("v", lambda e: e.tensor_scalar(nkeep, acc, 0.0, -1.0, A.is_le, A.mult), w=[("nb", 2, 3)], x=XA)
            elif k == "y0":
                op("v", lambda e: e.tensor_scalar(T.ec[:, 0:1], T.Kb[:, t + 1:t + 2], T.cb[:, 2:3], -1.0 / 128, A.subtract, A.mult),
                   r=[("Kb", t + 1, t + 2), ("cb", 2, 3)], w=[("ec", 0, 1)])
            elif k == "y1":
                op("p", lambda e: e.matmul(bank[ACC][0:1, 0:128], T.ec[:, 0:1], T.negI[:], True, True),
                   r=[("ec", 0, 1), ("negI", 0, 128)], x=XA)
            elif k == "y2":
                op("v", lambda e: e.tensor_copy(T.dif[0:1, :], bank[ACC][0:1, 0:128]), w=[("dif", 0, 128)], x=XA)
                op("y", lambda e: e.dma_start(T.ye[:], T.dif[0:1, :]), r=[("dif", 0, 128)], ch="stored", inc=16)
            elif k == "t":
                for i in range(it[2], it[3]):
                    tb, slot, _ = slot_of(step, i)
                    turn_block(T.h, "h", PAR["sets"][step][i][it[1]], tb, slot + it[1])
            elif k == "c":
                for i in range(it[1], it[2]):
                    tb, slot, at = slot_of(step, i)
                    compare(PAR["sets"][step][i][0], tb, slot, len(PAR["sets"][step][i]), at, -1.0)
            elif k == "n":
                for u in range(slot_of(step, it[1])[2], slot_of(step, it[2])[2], 128):
                    add_up(u)
            elif k == "r":
                op("v", lambda e, bi=it[1]: e.tensor_tensor_scan(T.run[:, 0:mw], bank[bi][:, 0:mw], T.run[:, 128:128 + mw], T.Kb[:, t:t + 1], A.add, A.add),
                   r=[("run", 128, 256), ("Kb", t, t + 1)], w=[("run", 0, mw)], x=["b%d" % it[1]])
            elif k == "j":
                into_sum(T.negI[:], T.run[:, mw - 1:mw], [("run", 0, mw), ("negI", 0, 128)])
            else:
                a, b = it[1], it[2]
                if k in ("gv", "gs", "tg"):
                    name = ("off%d", "land%d")[step] % rnd
                    rd = [("p", 0, W), (name, a // 16, b // 16)]
                    win = T.p[:, 0:W].indirect(T[name][:, a // 16:b // 16])
                    sc = -2.0 ** -shift_of(step, a)
                if k == "gv":
                    op("v", lambda e, a=a, b=b, win=win, sc=sc: e.tensor_scalar(T.h[:, a:b], win, sc, None, A.mult), r=rd, w=[("h", a, b)])
                elif k == "gs":
                    op("s", lambda e, a=a, b=b, win=win, sc=sc: e.activation(T.h[:, a:b], win, F.Copy, scale=sc), r=rd, w=[("h", a, b)])
                elif k == "tg":
                    op("v", lambda e, a=a, b=b, win=win: e.tensor_tensor(T.fb[:, a:b], win, T.ths[:, a:b], A.is_gt),
                       r=rd + [("ths", a, b)], w=[("fb", a, b)])
                elif k == "m":
                    for u in range(a, b, mw):
                        first, last = u == PAR["direct"][step][0], u + mw == PAR["direct"][step][1]
                        op("p", lambda e, u=u, first=first, last=last, bi=it[3]:
                           e.matmul(bank[bi][:, 0:mw], T.I[:, 128:256], T.fb[:, u:u + mw], first, last),
                           r=[("fb", u, u + mw), ("I", 128, 256)], x=["b%d" % it[3]])
                elif k == "pf":
                    fill(step, a, b, it[3])
                elif k == "pk":
                    kept(a, b, it[3])
                elif k == "cs":
                    op("s", lambda e, a=a, b=b, bi=it[3]: e.activation(T.p[:, a:b], bank[bi][:, 0:b - a], F.Copy, scale=unit),
                       r=[("sm", 8, 9)], w=[("p", a, b)], x=["b%d" % it[3]])
                elif k == "cv":
                    op("v", lambda e, a=a, b=b, bi=it[3]: e.tensor_scalar(T.p[:, a:b], bank[bi][:, 0:b - a], unit, None, A.mult),
                       r=[("sm", 8, 9)], w=[("p", a, b)], x=["b%d" % it[3]])
                elif k == "va":
                    op("v", lambda e, a=a, b=b: e.tensor_scalar(T.h[:, a:b], T.h[:, a:b], unit2, nkeep, A.mult, A.add),
                       r=[("h", a, b), ("nb", 0, 3)], w=[("h", a, b)])
                elif k == "vb":
                    op("v", lambda e, a=a, b=b: e.tensor_scalar(T.fb[:, a:b], T.p[:, a:b], nkeep, unit2, A.mult, A.subtract),
                       r=[("p", a, b), ("nb", 0, 3)], w=[("fb", a, b)])
                elif k == "vc":
                    op("v", lambda e, a=a, b=b: e.tensor_tensor_scan(T.p[:, a:b], T.h[:, a:b], T.fb[:, a:b], 1.0, A.min, A.mult),
                       r=[("fb", a, b), ("h", a, b)], w=[("p", a, b)])
                elif k == "ln":
                    op("s", lambda e, a=a, b=b, bi=it[3]: e.activation(T.lin[:, a:b], bank[bi][:, 0:b - a], F.Ln, scale=unit),
                       r=[("sm", 8, 9)], w=[("lin", a, b)], x=["b%d" % it[3]])
                elif k == "rs":
                    op("s", lambda e, a=a, b=b: e.activation(T.lin[:, a:b], T.lin[:, a:b], F.Identity, bias=MAGIC + MID, scale=1.0 / C),
                       r=[("lin", a, b)], w=[("lin", a, b)])
                elif k == "rv":
                    op("v", lambda e, a=a, b=b: e.tensor_scalar(T.lin[:, a:b], T.lin[:, a:b], 1.0 / C, MAGIC + MID, A.mult, A.add),
                       r=[("lin", a, b)], w=[("lin", a, b)])
                elif k == "sv":
                    op("v", lambda e, a=a, b=b: e.tensor_scalar(T.lin[:, a:b], T.lin[:, a:b], -MAGIC, None, A.add),
                       r=[("lin", a, b)], w=[("lin", a, b)])
                else:
                    op("y", lambda e, a=a, b=b: e.dma_start(T.yg[:, a:b], T.lin[:, a:b]), r=[("lin", a, b)], ch="stored", inc=16)

    if "only" in FOOT:
        key, t, it = FOOT["only"]
        del ops[:]
        keep = PAR[key]
        PAR[key] = [it]
        phase(key, (t + 1) // 2 if key[0] in "es" else t // 2, t)
        PAR[key] = keep
        return FOOT["hook"](ops)

    sub = PAR["sub"]
    into_sum(T.I[:, 0:128], T.cb[:, 2:3], [("I", 0, 128), ("cb", 2, 3)])
    pend = []
    for k in range(len(sub) - 1):
        a, b = sub[k], sub[k + 1]
        op("s", lambda e, a=a, b=b: e.activation(T.p[:, a:b], T.raw[:, a:b], F.Exp, bias=ENC, scale=C),
           r=[("raw", a, b)], w=[("p", a, b)])
        blocks = range(a // 128, (b + 127) // 128)
        for u in blocks:
            turn_block(T.p, "p", u, k % 2, u - a // 128)
        for u in pend:
            add_up(128 * u)
        for u in blocks:
            compare(u, k % 2, u - a // 128, 1, 128 * u, 1.0)
        pend = blocks
    for u in pend:
        add_up(128 * u)
    op("s", lambda e: e.activation(T.sm[:, 2:3], T.sm[:, 1:2], F.Ln), r=[("sm", 1, 2)], w=[("sm", 2, 3)])
    op("v", lambda e: e.tensor_scalar(T.rk[:], T.M16[:], acc, None, A.mult), r=[("M16", 0, 16)], w=[("rk", 0, 16)], x=XA)
    op("v", lambda e: e.tensor_copy(T.Kb[:, 0:1], acc), w=[("Kb", 0, 1)], x=XA)
    key1()
    key2(0)
    phase("e0", 0, -1)

    for rnd in range(RO):
        t = 2 * rnd
        phase("g0", rnd, t)
        phase("s0", rnd, t)
        phase("g1", rnd, t + 1)
        if rnd < RO - 1:
            phase("s1", rnd + 1, t + 1)

    phase("fin", None, 2 * RO - 1)
    FOOT["tag"] = None
    if "hook" in FOOT:
        return FOOT["hook"](ops)

    def meet(u, v):
        for (n1, a1, b1) in u:
            for (n2, a2, b2) in v:
                if n1 == n2 and a1 < b2 and a2 < b1:
                    return True
        return False

    known = {q: {} for q in Q}
    by_ch = {}
    clock = []
    waits = []
    marked = set()
    for i, o in enumerate(ops):
        q = o["q"]
        own = o["ch"] or q
        if q is None:
            clock.append({own: i})
            waits.append([])
            by_ch.setdefault(own, []).append(i)
            continue
        need = []
        for ch, lst in by_ch.items():
            same = o["ch"] is None and ch == q
            if same and q == "p":
                continue
            for j in reversed(lst):
                if known[q].get(ch, -1) >= j:
                    break
                e = ops[j]
                hit = meet(e["w"], o["r"]) or meet(e["w"], o["w"]) or meet(e["r"], o["w"])
                if hit or (not same and len(set(e["x"]) & set(o["x"])) > 0):
                    need.append(j)
                    break
        ws = []
        for j in sorted(need, reverse=True):
            if known[q].get(ops[j]["ch"] or ops[j]["q"], -1) >= j:
                continue
            ws.append(j)
            marked.add(j)
            for c2, j2 in clock[j].items():
                if known[q].get(c2, -1) < j2:
                    known[q][c2] = j2
        waits.append(ws)
        ck = dict(known[q])
        ck[own] = i
        clock.append(ck)
        by_ch.setdefault(own, []).append(i)

    semof = {"v": "cv", "s": "cs", "p": "cp", "g": "cg"}
    total = {}
    count = {}
    for i, o in enumerate(ops):
        if o["ch"] is not None or i in marked:
            name = o["ch"] or semof[o["q"]]
            total[name] = total.get(name, 0) + o["inc"]
            count[i] = (name, total[name])
    for i, o in enumerate(ops):
        if o["q"] is None:
            continue
        e = Q[o["q"]]
        for j in waits[i]:
            e.wait_ge(T.sem[count[j][0]], count[j][1])
        ins = o["fn"](e)
        if i in count and o["ch"] != "sent":
            ins.then_inc(T.sem[count[i][0]], o["inc"])
    g.wait_ge(T.sem.sent, total["sent"])
    g.sync.wait_ge(T.sem.stored, total["stored"])
